import numpy as np, ml_dtypes
CORES = [51,54,179,182]
N = 4
BF = ml_dtypes.bfloat16
def gentries(a):
    return np.ascontiguousarray(a.reshape(8, 16, -1).transpose(0, 2, 1)).reshape(8, -1)
def gtable(e):
    e = np.asarray(e); return np.ascontiguousarray(e.reshape(8, -1, 16).transpose(0, 2, 1)).reshape(128, -1).astype(np.int32)
S, RO, M, KS = 1280, 5, 32, 8192
W = N * S
def pair(o):
    p = np.empty(W, np.int64); p[o] = o[np.arange(W) ^ 1]; return p
def match(rng):
    return pair(rng.permutation(W))
def inside(rng):
    return pair(np.concatenate([q * S + rng.permutation(S) for q in range(N)]))
def across(rng):
    return pair(np.stack([np.arange(W // 2), W // 2 + rng.permutation(W // 2)], axis=1).reshape(-1))
def four(o, k):
    p = np.empty(W, np.int64); p[o.reshape(-1)] = o[:, np.arange(4) ^ k].reshape(-1); return p
def eights(rng):
    k = W // 8; i = np.arange(k); z = rng.permutation(np.arange(k, W - 2 * k)).reshape(k, 5)
    o = np.stack([z[:, 0], i, z[:, 1], W - 2 - 2 * i, W - 1 - 2 * i, z[:, 2], z[:, 3], z[:, 4]], axis=1)
    e = np.concatenate([np.full((k, 8), 16), rng.choice(np.array([4, 8, 12]), (k, 7)), np.ones((k, 1), np.int64)], axis=1)
    e = np.take_along_axis(e, np.argsort(rng.random((k, 16)), axis=1), 1)
    lo = rng.integers(0, M - 16, (k, 16)); hi = lo + e; one = lo + (e == 1)
    a = np.empty((16, W), np.int64); a[:, o.reshape(-1)] = np.stack([one, hi, hi, lo, lo, hi, hi, hi], axis=1).reshape(W, 16).T
    return pair(o.reshape(-1)), pair(np.roll(o, -1, axis=1).reshape(-1)), a
def parts(rng):
    share = rng.permutation(np.array([0.1, 0.2, 0.3, 0.5, 0.7, 1.0, 1.0, 1.0])).reshape(8, 1, 1)
    a = rng.integers(0, M, (8, 16, W)); b = np.where(rng.random((8, 16, W)) < share, rng.integers(0, M, (8, 16, W)), 0)
    return a, b, np.stack([match(rng) for g in range(8)]), np.stack([np.stack([match(rng) for t in range(RO)]) for g in range(8)])
def pack(a, b, lk, cd):
    side = lambda v: np.ascontiguousarray(v.reshape(128, N, S).transpose(1, 0, 2)).astype(np.float32).astype(BF)
    return {"x": side(a), "u": side(b), "link": np.stack([gtable(lk[:, q * S:(q + 1) * S]) for q in range(N)]),
            "cand": np.stack([gtable(cd[:, :, q * S:(q + 1) * S].reshape(8, RO * S)) for q in range(N)])}
def setup_inputs(rng):
    return pack(*parts(rng))
def setup_inputs_ties(rng):
    a, b, lk, cd = parts(rng)
    pa = rng.integers(0, M, (8, 16, 4)); pb = rng.integers(0, M, (8, 16, 4))
    pa[2:4] = 0; pa[2:4, 0, 2:] = 1; pb[2:4] = 0
    kind = np.broadcast_to(rng.integers(0, 4, (8, 1, W)), (8, 16, W))
    a[2:] = np.take_along_axis(pa, kind, 2)[2:]; b[2:] = np.take_along_axis(pb, kind, 2)[2:]
    for g in range(2):
        o = rng.permutation(W).reshape(W // 4, 4); lk[g] = four(o, 1)
        for t in range(RO): cd[g, t] = four(o, (2, 3, 1)[t % 3])
    return pack(a, b, lk, cd)
def setup_inputs_again(rng):
    a, b, lk, cd = parts(rng); b = rng.integers(0, 2, b.shape)
    for g in (0, 1): cd[g, 1:] = cd[g, :1]
    for g in (2, 3): cd[g, 0] = lk[g]
    for g in (4, 5): cd[g, 2:] = cd[g, np.arange(2, RO) % 2]
    for g in (6, 7):
        o = rng.permutation(W); lk[g] = pair(o); h = W // 2
        for t in range(RO): cd[g, t] = pair(np.concatenate([o[:h], rng.permutation(o[h:])]))
    return pack(a, b, lk, cd)
def setup_inputs_places(rng):
    a, b, lk, cd = parts(rng); v = np.arange(W)
    lk[0] = v ^ 1; lk[1] = W - 1 - v; lk[2] = (v + W // 2) % W; lk[3] = inside(rng); lk[4] = inside(rng); lk[5] = across(rng)
    for t in range(RO):
        cd[0, t] = W - 1 - v if t % 2 == 0 else v ^ 2
        cd[1, t] = v ^ (1 << (t % 4)); cd[2, t] = inside(rng); cd[3, t] = inside(rng); cd[4, t] = across(rng); cd[5, t] = across(rng)
    o = np.concatenate([np.stack([q * S + rng.permutation(S) for q in four_ranks], axis=1) for four_ranks in rng.permutation(N).reshape(N // 4, 4)])
    lk[7] = four(o, 1); cd[7, 0] = four(o, 2); cd[7, 1] = cd[7, 0]
    p = rng.integers(0, M, (W // 4, 16)); e = (p + rng.integers(M // 4, M - M // 4 + 1, (W // 4, 16))) & (M - 1)
    a[7][:, o.reshape(-1)] = np.stack([p, e, p, e], axis=1).reshape(W, 16).T
    b[6] = rng.integers(0, M, (16, W))
    return pack(a, b, lk, cd)
def setup_inputs_far(rng):
    a, b, lk, cd = parts(rng); v = np.arange(W)
    for g in range(8):
        flip = (rng.random(W) < 0.5)[np.minimum(v, lk[g])]
        s = flip if g % 2 else flip ^ (v < lk[g])
        a[g] = np.where(s, 16, 0)[None, :]
        b[g] = rng.choice(np.array([0, 16]), W)[None, :]
    lk[3], cd[3, 1], a[3] = eights(rng)
    lk[4], last, a[4] = eights(rng); b[4] = 0; cd[4, 1:RO - 1] = lk[4]; cd[4, RO - 1] = last
    o = np.concatenate([np.arange(W // 2).reshape(W // 4, 2), (W // 2 + rng.permutation(W // 2)).reshape(W // 4, 2)], axis=1)
    lk[6] = four(o, 1); cd[6, 1] = four(o, 2); s = np.zeros(W, bool)
    s[o.reshape(-1)] = ((rng.random((W // 4, 1)) < 0.5) ^ (np.arange(4) % 2 == 1)[None, :]).reshape(-1)
    a[6] = np.where(s, 16, 0)[None, :]
    a[7] = rng.integers(0, M, (16, 1)); b[7] = 0
    cd[:, 0] = lk
    return pack(a, b, lk, cd)
def setup_inputs_spread(rng):
    a, b, lk, cd = parts(rng)
    a = np.minimum((np.exp2(5 * rng.random((8, 1, W))) * rng.random(a.shape) * 1.25).astype(np.int64), M - 1)
    b = np.minimum((np.exp2(5 * rng.random((8, 1, W))) * rng.random(b.shape) ** 2).astype(np.int64), M - 1) * (rng.random((8, 1, W)) < 0.75)
    return pack(a, b, lk, cd)
def joined(a, n):
    e = np.stack([gentries(b) for b in a]).astype(np.int64).reshape(N, 8, n, S)
    return np.ascontiguousarray(e.transpose(1, 2, 0, 3)).reshape(8, n, W)
def check_inputs(d):
    bad = []
    for k in ("x", "u"):
        a = np.asarray(d[k]).astype(np.float32)
        if not np.all((a >= 0) & (a <= M - 1) & (a == np.floor(a))): bad.append("range of " + k)
    for k, n in (("link", 1), ("cand", RO)):
        a = np.asarray(d[k])
        if np.min(a) < 0 or np.max(a) > W - 1: bad.append("range of " + k); continue
        e = joined(a, n); v = np.arange(W)
        if np.any(e == v): bad.append("a satellite paired with itself in " + k)
        if np.any(np.take_along_axis(e, e, 2) != v): bad.append("pairs of " + k)
    return bad
def pick(a, i):
    return np.take_along_axis(a, i, 1) if a.ndim == 2 else np.take_along_axis(a, i[:, None, :], 2)
def cost(a, b):
    e = np.abs(a - b)
    return np.add.reduce(np.minimum(e, M - e), axis=1)
def reference(x, u, link, cand):
    xs, us = [np.ascontiguousarray(a.astype(np.float32).astype(np.int64).transpose(1, 0, 2)).reshape(8, 16, W) for a in (x, u)]
    lk = joined(link, 1)[:, 0]; cd = joined(cand, RO); v = np.arange(W)
    for t in range(RO):
        b = lk; c = cd[:, t]; d = pick(lk, c)
        xb = pick(xs, b); xc = pick(xs, c); xd = pick(xs, d)
        g = cost(xs, xb) + cost(xc, xd) - cost(xs, xc) - cost(xb, xd)
        key = KS * g - np.minimum(v, c)
        go = (g > 0) & (key > pick(key, b)) & (key > pick(key, d))
        new = np.where(go, c, np.where(pick(go, b), pick(d, b), b))
        ch = np.roll(new != lk, -1, axis=0).astype(np.int64)
        xs = (xs + us * ch[:, None, :]) & (M - 1)
        lk = new
    return {"ylink": np.stack([gtable(lk[:, q * S:(q + 1) * S]) for q in range(N)]).astype(np.float32)}

@@ -1,0 +1,462 @@
+from concourse.bass import DstId, RemoteDMATransfer
+from concourse.mybir import AluOpType as A, ActivationFunctionType as F
+
+N, S, RO, W, K = 4, 1280, 5, 5120, 80
+CH = [(0, 512), (512, 1024), (1024, 1280)]
+LW = 2 * W + K
+
+
+def _sb(dtype, **kw):
+    return {k: ("sbuf", [128, n], dtype) for k, n in kw.items()}
+
+
+SCRATCH = {
+    **_sb("bfloat16", xraw=S, uraw=S, xt=RO * W, ut=W, xc=W, xv=S, lt=LW, kt=W, sg=2 * S, lg=S, kg=3 * S, yb=S, yc=S, xd=S,
+          p1=S, c1=S, p2=S, c2=S, p3=S, c3=S, p4=S, c4=S, vd=2 * K, bp=144, bm=144, bl=144, bk=144, ip=128, im=128, sh=128,
+          mh=RO * K, ml=RO * K, lm=RO * 2 * K, dm=RO * 2 * K, km=RO * K, go=RO * 2 * K),
+    **_sb("int32", li=K, ci=RO * K, rowi=128, rowj=128, pi=8, t1=RO * K, t2=RO * K),
+    **_sb("float32", row=144, vk=K, vf=K, pf=32, cf=RO * K, mf=RO * K, t3=RO * K, t4=RO * K, t5=RO * K, t6=RO * K,
+          nb=(RO + 1) * K, de=2 * K, s=12 * K),
+    **_sb("uint16", cn=RO * K, cp=RO * K, bn=K, dn=K, ko=3 * K, av=RO * N * K),
+    "ld": ("dram", [RO * N, 128, 2 * K], "bfloat16"), "dd": ("dram", [RO * N * 2, 128, K], "bfloat16"),
+    "md": ("dram", [RO * N * 2, 128, K], "bfloat16"), "kd": ("dram", [RO * N, 128, K], "bfloat16"),
+    "pa": ("psum", [128, 1536], "float32"), "pb": ("psum", [128, 1536], "float32"),
+    "pg": ("psum", [128, 512], "float32"), "pv": ("psum", [128, 512], "float32"),
+}
+SEMAPHORES = (["V", "S", "P", "G", "ls", "ldl", "ldc", "ldx0", "ldx1", "ldu", "dl", "dd", "dm", "dk", "out",
+               "xs0", "xs1", "xf0", "xf1", "xw0", "xw1", "us", "uf", "uw"]
+              + ["%s%d_%d" % (k, t, q) for k in "almdk" for t in range(RO) for q in range(N)])
+
+
+def rank_program(g, core, T, topo):
+    q = T.rank_of(core)
+    if q is None:
+        return
+    cores = T.cores
+    same = lambda a, b: topo.host(a) == topo.host(b) and topo.chip(a) == topo.chip(b)
+    sib = [r for r in range(N) if r != q and same(cores[r], core)][0]
+    far = [r for r in range(N) if not same(cores[r], core)]
+    f0 = [r for r in far if topo.die(cores[r]) == topo.die(core)][0]
+    f1 = [r for r in far if r != f0][0]
+    peers = [sib, f0, f1]
+    fe = topo.engines(core, cores[f0])
+    se = [e for e in topo.engines(core, cores[sib]) if e not in fe]
+    msk = lambda es: sum(1 << e for e in es)
+    dst = lambda r: DstId(rid=topo.addr(cores[r], core)[0], pnc=topo.addr(cores[r], core)[1])
+
+    Q = {"V": g.vector, "S": g.scalar, "P": g.tensor, "G": g, "Y": g.sync}
+    cnt = {}
+    waited = {k: {} for k in Q}
+    wr, rd, bank = {}, {}, {}
+
+    def wait(e, toks):
+        need = {}
+        for s_, v in toks:
+            need[s_] = max(need.get(s_, 0), v)
+        for s_, v in need.items():
+            if waited[e].get(s_, 0) < v:
+                Q[e].wait_ge(T.sem[s_], v)
+                waited[e][s_] = v
+
+    def deps(e, r, w, banks=()):
+        toks = []
+        for x in r:
+            toks += wr[x]
+        for x in w:
+            toks += [k for k in wr.get(x, []) if k[0] != e] + rd.get(x, [])
+        for b in banks:
+            toks += [k for k in bank.get(b, {}).values() if k[0] != e]
+        return toks
+
+    def done(tok, r, w, banks=()):
+        for x in r:
+            rd.setdefault(x, []).append(tok)
+        for x in w:
+            wr[x] = [tok]
+            rd[x] = []
+        for b in banks:
+            bank.setdefault(b, {})[tok[0]] = tok
+
+    def op(e, fn, r, w, banks=()):
+        wait(e, deps(e, r, w, banks))
+        cnt[e] = cnt.get(e, 0) + 1
+        fn().then_inc(T.sem[e], 1)
+        done((e, cnt[e]), r, w, banks)
+
+    def ts(out, in0, s1, s2, o0, o1, r, w, banks=()):
+        if s2 is None:
+            op("V", lambda: g.vector.tensor_scalar(out, in0, s1, None, o0), r, w, banks)
+        else:
+            op("V", lambda: g.vector.tensor_scalar(out, in0, s1, s2, o0, o1), r, w, banks)
+
+    def tt(out, a, b, o, r, w, banks=()):
+        op("V", lambda: g.vector.tensor_tensor(out, a, b, o), r, w, banks)
+
+    def cp(out, a, r, w, banks=()):
+        op("V", lambda: g.vector.tensor_copy(out, a), r, w, banks)
+
+    def fill(out, v, w):
+        op("V", lambda: g.vector.memset(out, v), [], w)
+
+    def act(out, a, f, r, w, banks=(), **kw):
+        op("S", lambda: g.scalar.activation(out, a, f, **kw), r, w, banks)
+
+    def mm(items, r, w, banks):
+        def fn():
+            last = None
+            for it in items:
+                last = g.tensor.matmul(*it)
+            return last
+        op("P", fn, r, w, banks)
+
+    def fold(out, B, src, c0, first, last, r, w, b):
+        mm([(out, B[:, 15 - i:143 - i], src[:, c0 + i:c0 + S:16], first and i == 0, last and i == 15) for i in range(16)],
+           r, w, [b])
+
+    def dmas(sem, items, w, e="Y"):
+        wait(e, deps(e, [], w))
+        for o, i, r in items:
+            wait(e, deps(e, r, []))
+            Q[e].dma_start(o, i).then_inc(T.sem[sem], 16)
+            cnt[sem] = cnt.get(sem, 0) + 16
+        done((sem, cnt[sem]), [], w)
+
+    def send(trs, r):
+        wait("G", deps("G", r, []))
+        g.remote_dma_fused([RemoteDMATransfer(dst_ids=[dst(p)], dma_engine_mask=msk(es), remote_sem=T.sem[sm], src=a, dst=b)
+                            for p, es, sm, a, b in trs], local_sem=T.sem.ls)
+        cnt["ls"] = cnt.get("ls", 0) + sum(len(x[1]) for x in trs)
+
+    hf = len(fe) // 2
+    share = {sib: se, f0: fe[:hf], f1: fe[hf:]}
+
+    def allsend(kind, t, pairs, r):
+        trs = []
+        for p in peers:
+            n = len(share[p]) // len(pairs)
+            for i, (a, b) in enumerate(pairs):
+                trs.append((p, share[p][i * n:(i + 1) * n], "%s%d_%d" % (kind, t, q), a, b))
+        send(trs, r)
+        for p in peers:
+            nm = "%s%d_%d" % (kind, t, p)
+            wr[nm] = [(nm, len(share[p]))]
+
+    def place(src, n, out, res, wres, mul, base):
+        ts(T.t1[:, :n], src, 1.0 / 16, -0.46875, A.mult, A.add, res, ["t1"])
+        ts(T.t2[:, :n], src, 1.0 / S, -0.4996, A.mult, A.add, res, ["t2"])
+        ts(T.t3[:, :n], src, float(mul), float(base), A.mult, A.add, res, ["t3"])
+        ts(T.t4[:, :n], T.t1[:, :n], float(1 - 16 * mul), None, A.mult, None, ["t1"], ["t4"])
+        ts(T.t5[:, :n], T.t2[:, :n], float(16 * mul - K), None, A.mult, None, ["t2"], ["t5"])
+        tt(T.t6[:, :n], T.t3[:, :n], T.t4[:, :n], A.add, ["t3", "t4"], ["t6"])
+        tt(T.t3[:, :n], T.t6[:, :n], T.t5[:, :n], A.add, ["t6", "t5"], ["t3"])
+        cp(out, T.t3[:, :n], ["t3"], wres)
+
+    blk = lambda buf, n, p: buf[:, n * W + p * S:n * W + (p + 1) * S]
+    PS = {"a": T.pa, "b": T.pb}
+    banks3 = lambda z: [z + "0", z + "1", z + "2"]
+    so = {"a": 0, "b": S}
+
+    def tab_pe(n, p, z, minus=None):
+        it = []
+        for a, b in CH:
+            o = n * W - W + p * S
+            it.append((PS[z][:, a:b], T.ip[:], T.xt[:, o + a:o + b], True, False))
+            it.append((PS[z][:, a:b], T.ip[:], T.ut[:, p * S + a:p * S + b], False, minus is None))
+            if minus:
+                it.append((PS[z][:, a:b], T.im[:], T.sg[:, so[minus] + a:so[minus] + b], False, True))
+        mm(it, ["ip", "xt%d_%d" % (n - 1, p), "ut%d" % p] + (["im", "sg" + minus] if minus else []), ["ps" + z], banks3(z))
+
+    def tab_s(z):
+        act(T.sg[:, so[z]:so[z] + S], PS[z][:, :S], F.Sign, ["ps" + z], ["sg" + z], banks3(z), bias=T.pf[:, 28:29])
+
+    def tab_v(n, p, z):
+        tt(blk(T.xt, n, p), PS[z][:, :S], T.sg[:, so[z]:so[z] + S], A.subtract, ["ps" + z, "sg" + z],
+           ["xt%d_%d" % (n, p)], banks3(z))
+
+    def link_msg(t):
+        nb = T.nb[:, t * K:(t + 1) * K]
+        hi = T.lm[:, 2 * t * K:(2 * t + 1) * K]
+        cp(hi, nb, ["nb%d" % t], ["lh%d" % t])
+        tt(T.lm[:, (2 * t + 1) * K:(2 * t + 2) * K], nb, hi, A.subtract, ["nb%d" % t, "lh%d" % t], ["ll%d" % t])
+        allsend("l", t, [(T.lm[:, 2 * t * K:(2 * t + 2) * K], T.ld[t * N + q])], ["lh%d" % t, "ll%d" % t])
+
+    def link_table(t):
+        it = []
+        for p in [q] + peers:
+            src = T.lm[:, 2 * t * K:(2 * t + 2) * K] if p == q else T.ld[t * N + p]
+            r = ["lh%d" % t, "ll%d" % t] if p == q else ["l%d_%d" % (t, p)]
+            for h in range(2):
+                o = K - h * K + p * 2 * S
+                it.append((T.lt[h::16, o:o + 2 * S], src, r))
+        dmas("dl", it, ["lt"])
+
+    def two_send(kind, t, a, b, dram, r):
+        allsend(kind, t, [(a, dram[(t * N + q) * 2]), (b, dram[(t * N + q) * 2 + 1])], r)
+
+    def two_table(kind, t, a, b, dram, r0, tab, h0, sem, w):
+        it = []
+        for p in [q] + peers:
+            for h in range(2):
+                src = (a, b)[h] if p == q else dram[(t * N + p) * 2 + h]
+                it.append((tab[h0 + h::16, p * S:(p + 1) * S], src, r0 if p == q else ["%s%d_%d" % (kind, t, p)]))
+        dmas(sem, it, w)
+
+    mpair = lambda t: (T.mh[:, t * K:(t + 1) * K], T.ml[:, t * K:(t + 1) * K])
+    sm = lambda i: T.s[:, i * K:(i + 1) * K]
+    pd, pe_, kb, kd, ke = [T.pg[:, i * K:(i + 1) * K] for i in range(5)]
+    pgn, pav = T.pv[:, :K], T.pv[:, K:2 * K]
+    one = T.pf[:, 20:21]
+
+    def link_lookup(t):
+        act(T.lg[:], T.lt[:, :].indirect(T.cp[:, t * K:(t + 1) * K]), F.Copy, ["lt", "cp0" if t == 0 else "cp"], ["lg"])
+        fold(pd, T.bl, T.lg, 0, True, True, ["bl", "lg"], ["pd"], "g")
+
+    def d_rest(t):
+        hi, lo = T.dm[:, 2 * t * K:(2 * t + 1) * K], T.dm[:, (2 * t + 1) * K:(2 * t + 2) * K]
+        cp(hi, pd, ["pd"], ["dh%d" % t], ["g"])
+        cp(T.de[:, :K], pd, ["pd"], ["de0"], ["g"])
+        tt(lo, pd, hi, A.subtract, ["pd", "dh%d" % t], ["dlo%d" % t], ["g"])
+        r = ["dh%d" % t, "dlo%d" % t]
+        two_send("d", t, hi, lo, T.dd, r)
+        two_table("d", t, hi, lo, T.dd, r, T.lt, 0, "dd", ["lt"])
+
+    H = S // 2
+    dmas("ldl", [(T.li[:], T.link[:], [])], ["li"], "S")
+    dmas("ldx0", [(T.xraw[:, :H], T.x[:, :H], [])], ["xr0"])
+    dmas("ldx1", [(T.xraw[:, H:], T.x[:, H:], [])], ["xr1"], "S")
+    dmas("ldc", [(T.ci[:], T.cand[:], [])], ["ci"])
+    dmas("ldu", [(T.uraw[:], T.u[:], [])], ["ur"])
+    op("G", lambda: g.iota(T.pi[:, 0:1], [[0, 1]], 0, 1), [], ["pi0"])
+    op("G", lambda: g.iota(T.row[:], [[1, 144]], -15, 0, allow_small_or_imprecise_dtypes=True), [], ["row"])
+    op("G", lambda: g.iota(T.rowi[:], [[1, 128]], 16, 0), [], ["rowi"])
+    op("G", lambda: g.iota(T.vk[:], [[16, K]], q * S, 0, allow_small_or_imprecise_dtypes=True), [], ["vk"])
+
+    L1 = 4096
+    fill(T.lt[:, :L1], 0.0, ["lt_a"])
+    cp(T.nb[:, :K], T.li[:], ["li"], ["nb0"])
+    link_msg(0)
+    for h in range(2):
+        own = T.xt[:, q * S + h * H:q * S + (h + 1) * H]
+        act(own, T.xraw[:, h * H:(h + 1) * H], F.Copy, ["xr%d" % h], ["xo%d" % h], scale=1.0 / 16)
+        send([(sib, se, "xs%d" % h, own, own), (f0, fe, "xf%d" % h, own, own)], ["xo%d" % h])
+    wr["xt0_%d" % q] = wr["xo1"]
+    wr["xt0_%d" % sib] = [("xs0", len(se)), ("xs1", len(se))]
+    wr["xt0_%d" % f0] = [("xf0", len(fe)), ("xf1", len(fe))]
+    wr["xt0_%d" % f1] = [("xw0", len(se)), ("xw1", len(se))]
+    fill(T.pf[:, 28:29], -31.0 / 32, ["pfs"])
+    fill(one, 1.0, ["pf1"])
+    uo = blk(T.ut, 0, q)
+    ts(uo, T.uraw[:], 1.0 / 16, -1.0, A.mult, A.add, ["ur"], ["ut%d" % q])
+    send([(sib, se, "us", uo, uo), (f0, fe, "uf", uo, uo)], ["ut%d" % q])
+    wr["ut%d" % sib] = [("us", len(se))]
+    wr["ut%d" % f0] = [("uf", len(fe))]
+    wr["ut%d" % f1] = [("uw", len(se))]
+    for h in range(2):
+        wait("G", [("xf%d" % h, len(fe))])
+        a = T.xt[:, f0 * S + h * H:f0 * S + (h + 1) * H]
+        send([(sib, se, "xw%d" % h, a, a)], [])
+    fill(T.lt[:, L1:], 0.0, ["lt"])
+    link_table(0)
+    for p in range(N):
+        act(T.kt[:, p * S:(p + 1) * S], T.xraw[:], F.Copy, ["xr0", "xr1"], ["ktm", "ktk"])
+    ts(T.pi[:, 4:5], T.pi[:, 0:1], 15, None, A.bitwise_and, None, ["pi0"], ["pi4"])
+    cp(T.pf[:, 0:1], T.pi[:, 0:1], ["pi0"], ["p"])
+    cp(T.cf[:], T.ci[:], ["ci"], ["cf"])
+    cp(T.pf[:, 4:5], T.pi[:, 4:5], ["pi4"], ["pm"])
+    ts(T.ip[:], T.row[:, 15:143], T.pf[:, 0:1], None, A.is_equal, None, ["row", "p"], ["ip"])
+    ts(T.im[:], T.row[:, 15:143], T.pf[:, 0:1], -1.0, A.is_equal, A.mult, ["row", "p"], ["im"])
+    tt(T.pf[:, 8:9], T.pf[:, 0:1], T.pf[:, 4:5], A.subtract, ["p", "pm"], ["g16"])
+    ts(T.pf[:, 12:13], T.pf[:, 4:5], 2.0, None, A.is_lt, None, ["pm"], ["wl"])
+    place(T.cf[:, :K], K, T.cp[:, :K], ["cf"], ["cp0"], 2 * K, K)
+    ts(T.bl[:], T.row[:], T.pf[:, 8:9], T.pf[:, 12:13], A.is_equal, A.mult, ["row", "g16", "wl"], ["bl"])
+    wait("S", wr["pfs"] + wr["pf1"])
+    tab_pe(1, q, "b")
+    tab_s("b")
+    link_lookup(0)
+    ts(T.pf[:, 13:14], T.pf[:, 4:5], 0.0, 16385.0, A.is_equal, A.mult, ["pm"], ["wk0"])
+    ts(T.pf[:, 14:15], T.pf[:, 4:5], 3.0, None, A.is_lt, None, ["pm"], ["wk1"])
+    ts(T.vf[:], T.vk[:], T.pf[:, 4:5], None, A.add, None, ["vk", "pm"], ["vf"])
+    ts(T.rowj[:], T.rowi[:], 127, None, A.bitwise_and, None, ["rowi"], ["rowj"])
+    tt(T.pf[:, 16:17], T.pf[:, 13:14], T.pf[:, 14:15], A.subtract, ["wk0", "wk1"], ["wk"])
+    for t in range(RO):
+        tt(T.mf[:, t * K:(t + 1) * K], T.cf[:, t * K:(t + 1) * K], T.vf[:], A.min, ["cf", "vf"], ["mf"])
+    tab_v(1, q, "b")
+    cp(T.mh[:], T.mf[:], ["mf"], ["mh"])
+    cp(T.cn[:], T.ci[:], ["ci"], ["cn"])
+    tt(T.ml[:], T.mf[:], T.mh[:], A.subtract, ["mf", "mh"], ["ml"])
+    two_send("m", 0, *mpair(0), T.md, ["mh", "ml"])
+    two_table("m", 0, *mpair(0), T.md, ["mh", "ml"], T.kt, 1, "dm", ["ktm"])
+    tab_pe(2, q, "a")
+    tab_s("a")
+    tab_pe(2, q, "b", "a")
+    act(blk(T.xt, 2, q), T.pb[:, :S], F.Copy, ["psb"], ["xt2_%d" % q], banks3("b"))
+    cp(T.bn[:], T.li[:], ["li"], ["bn"])
+    ts(T.xv[:], T.xraw[:], 1.0 / 16, None, A.mult, None, ["xr0", "xr1"], ["xv"])
+    ts(T.bp[:], T.row[:], T.pf[:, 8:9], 16.0, A.is_equal, A.mult, ["row", "g16"], ["bp"])
+    ts(T.bm[:], T.row[:], T.pf[:, 8:9], -16.0, A.is_equal, A.mult, ["row", "g16"], ["bm"])
+    ts(T.bk[:], T.row[:], T.pf[:, 8:9], T.pf[:, 16:17], A.is_equal, A.mult, ["row", "g16", "wk"], ["bk"])
+    ts(T.sh[:], T.rowj[:], T.pf[:, 0:1], float(W), A.is_equal, A.mult, ["rowj", "p"], ["sh"])
+    cp(T.vd[:, :K], T.vf[:], ["vf"], ["vh"])
+    cp(T.dn[:], pd, ["pd"], ["dn"], ["g"])
+    d_rest(0)
+    tt(T.vd[:, K:], T.vf[:], T.vd[:, :K], A.subtract, ["vf", "vh"], ["vl"])
+    place(T.nb[:, :K], K, T.ko[:, :K], ["nb0"], ["ko0"], K, 0)
+    place(T.cf[:, K:], (RO - 1) * K, T.cp[:, K:], ["cf"], ["cp"], 2 * K, K)
+    tab_pe(1, sib, "a")
+    tab_s("a")
+    tab_pe(3, q, "b")
+    tab_s("b")
+    tab_v(1, sib, "a")
+    tab_v(3, q, "b")
+    wait("G", [("uf", len(fe))])
+    a = blk(T.ut, 0, f0)
+    send([(sib, se, "uw", a, a)], [])
+    todo = [[(1, f0), (1, f1), (2, sib)], [(2, f0), (2, f1), (3, sib)], [(3, f0), (3, f1), (4, q)], [(4, sib), (4, f0), (4, f1)]]
+
+    for t in range(RO):
+        nb = T.nb[:, t * K:(t + 1) * K]
+        last = t == RO - 1
+        if t == 0:
+            X, xr = T.xt, ["xt0_%d" % p for p in range(N)]
+        else:
+            X, xr = T.xc, ["xc_own", "xc_V", "xc_S"]
+            cols = [c for p in range(N) if p != q for c in range(p * K, (p + 1) * K)]
+            tabs = ["xt%d_%d" % (n, p) for n in range(t + 1) for p in range(N)]
+            for e, part in (("V", cols[:len(cols) // 2]), ("S", cols[len(cols) // 2:])):
+                runs = []
+                for c in part:
+                    if runs and runs[-1][1] == c:
+                        runs[-1][1] = c + 1
+                    else:
+                        runs.append([c, c + 1])
+                for a, b in runs:
+                    src = T.xt[:, :(t + 1) * W].indirect(T.av[:, t * N * K + a:t * N * K + b])
+                    r = tabs + ["a%d_%d" % (t, p) for p in range(a // K, (b - 1) // K + 1)]
+                    if e == "V":
+                        cp(T.xc[:, 16 * a:16 * b], src, r, ["xc_V"])
+                    else:
+                        act(T.xc[:, 16 * a:16 * b], src, F.Copy, r, ["xc_S"])
+            link_lookup(t)
+        win = X[:, :W]
+        tt(T.yb[:], win.indirect(T.bn[:]), T.xv[:], A.subtract, xr + ["bn", "xv"], ["yb"])
+        ck = t * K
+        if t == 0:
+            tt(T.yc[:], win.indirect(T.cn[:, ck:ck + K]), T.xv[:], A.subtract, xr + ["cn", "xv"], ["yc"])
+        else:
+            tt(T.yc[:, :H], win.indirect(T.cn[:, ck:ck + K // 2]), T.xv[:, :H], A.subtract, xr + ["cn", "xv"], ["yc"])
+            act(T.p1[:], T.yb[:], F.Relu, ["yb"], ["p1"], bias=one)
+            cp(T.dn[:], pd, ["pd"], ["dn"], ["g"])
+            tt(T.yc[:, H:], win.indirect(T.cn[:, ck + K // 2:ck + K]), T.xv[:, H:], A.subtract, xr + ["cn", "xv"], ["yc"])
+        for i, (a, b) in enumerate(CH):
+            act(T.xd[:, a:b], win.indirect(T.dn[:, a // 16:b // 16]), F.Copy, xr + ["dn"], ["xd%d" % i])
+        if t == 0:
+            act(T.p1[:], T.yb[:], F.Relu, ["yb"], ["p1"], bias=one)
+        else:
+            d_rest(t)
+        for z, y, yr in (("b", T.yb, "yb"), ("a", T.yc, "yc")):
+            it = []
+            for a, b in CH:
+                it.append((PS[z][:, a:b], T.ip[:], T.xv[:, a:b], True, False))
+                it.append((PS[z][:, a:b], T.ip[:], y[:, a:b], False, False))
+            mm(it, ["ip", yr, "xv"], ["ps" + z], banks3(z))
+            if z == "b" and t > 0:
+                fold(pgn, T.bm, T.p1, 0, True, False, ["bm", "p1"], ["pgn"], "v")
+        ts(T.p3[:], T.yc[:], -1.0, None, A.max, None, ["yc"], ["p3"])
+        ts(T.c3[:], T.yc[:], 0.0, 1.0, A.max, A.min, ["yc"], ["c3"])
+        ts(T.c1[:], T.p1[:], 1.0, 2.0, A.max, A.min, ["p1"], ["c1"])
+        for i, (a, b) in enumerate(CH):
+            for z in "ba":
+                mm([(PS[z][:, a:b], T.im[:], T.xd[:, a:b], False, True)], ["im", "xd%d" % i], ["e%s%d" % (z, i)], [z + str(i)])
+            if i == 0:
+                fold(pgn, T.bp, T.p3, 0, t == 0, False, ["bp", "p3"], ["pgn"], "v")
+            if i == 1:
+                fold(pgn, T.bm, T.c3, 0, False, False, ["bm", "c3"], ["pgn"], "v")
+        if t == 0:
+            fold(pgn, T.bm, T.p1, 0, False, False, ["bm", "p1"], ["pgn"], "v")
+        fold(pgn, T.bp, T.c1, 0, False, False, ["bp", "c1"], ["pgn"], "v")
+        a, b = CH[0]
+        ts(T.p4[:, a:b], T.pb[:, a:b], -1.0, None, A.max, None, ["eb0"], ["p4_0"], ["b0"])
+        ts(T.c4[:, a:b], T.p4[:, a:b], 0.0, 1.0, A.max, A.min, ["p4_0"], ["c4_0"])
+        for z, i in (("b", 1), ("b", 2), ("a", 0), ("a", 1), ("a", 2)):
+            a, b = CH[i]
+            pz, cz, nm = (T.p4, T.c4, "4_%d" % i) if z == "b" else (T.p2, T.c2, "2_%d" % i)
+            act(pz[:, a:b], PS[z][:, a:b], F.Relu, ["e%s%d" % (z, i)], ["p" + nm], [z + str(i)], bias=one)
+            ts(cz[:, a:b], pz[:, a:b], 1.0, 2.0, A.max, A.min, ["p" + nm], ["c" + nm])
+            if (z, i) == ("b", 2):
+                fold(pgn, T.bp, T.p4, 0, False, False, ["bp", "p4_0", "p4_1", "p4_2"], ["pgn"], "v")
+                fold(pgn, T.bm, T.c4, 0, False, False, ["bm", "c4_0", "c4_1", "c4_2"], ["pgn"], "v")
+        fold(pgn, T.bm, T.p2, 0, False, False, ["bm", "p2_0", "p2_1", "p2_2"], ["pgn"], "v")
+        fold(pgn, T.bp, T.c2, 0, False, True, ["bp", "c2_0", "c2_1", "c2_2"], ["pgn"], "v")
+        km = T.km[:, ck:ck + K]
+        ts(km, pgn, 0.0, None, A.max, None, ["pgn"], ["km%d" % t], ["v"])
+        allsend("k", t, [(km, T.kd[t * N + q])], ["km%d" % t])
+        dmas("dk", [(T.kt[0::16, p * S:(p + 1) * S], km if p == q else T.kd[t * N + p],
+                     ["km%d" % t] if p == q else ["k%d_%d" % (t, p)]) for p in [q] + peers], ["ktk"])
+        act(T.lg[:], T.lt[:, :W].indirect(T.ko[:, :K]), F.Copy, ["lt", "ko0"], ["lg"])
+        if not last:
+            tab_pe(*todo[t][0], "b")
+        fold(pe_, T.bl, T.lg, 0, True, True, ["bl", "lg"], ["pe"], "g")
+        if not last:
+            tab_pe(*todo[t][1], "a")
+            tab_s("b")
+            tab_s("a")
+        ts(sm(11), km, 16384.0, None, A.mult, None, ["km%d" % t], ["s11"])
+        ts(sm(1), km, 32768.0, -6000.0, A.mult, A.add, ["km%d" % t], ["s1"])
+        tt(sm(4), T.cf[:, ck:ck + K], nb, A.subtract, ["cf", "nb%d" % t], ["s4"])
+        tt(sm(0), sm(11), T.mf[:, ck:ck + K], A.subtract, ["s11", "mf"], ["s0"])
+        cp(T.de[:, K:], pe_, ["pe"], ["de1"], ["g"])
+        ts(sm(2), sm(0), 0.0, None, A.max, None, ["s0"], ["s2"])
+        tt(sm(3), sm(0), sm(1), A.min, ["s0", "s1"], ["s3"])
+        tt(sm(5), T.de[:, K:], nb, A.subtract, ["de1", "nb%d" % t], ["s5"])
+        place(T.de[:], 2 * K, T.ko[:, K:], ["de0", "de1"], ["ko1"], K, 0)
+        if not last:
+            tab_v(*todo[t][0], "b")
+            tab_pe(*todo[t][2], "b")
+            tab_v(*todo[t][1], "a")
+            tab_s("b")
+        kr = ["ktm", "ktk", "ko0", "ko1"]
+        kw = T.kt[:, :]
+        cp(T.kg[:, :S], kw.indirect(T.ko[:, :K]), kr, ["kg0"])
+        act(T.kg[:, S:2 * S], kw.indirect(T.ko[:, K:2 * K]), F.Copy, kr, ["kg1"])
+        cp(T.kg[:, 2 * S:2 * S + H], kw.indirect(T.ko[:, 2 * K:2 * K + K // 2]), kr, ["kg2"])
+        act(T.kg[:, 2 * S + H:], kw.indirect(T.ko[:, 2 * K + K // 2:]), F.Copy, kr, ["kg3"])
+        fold(kb, T.bk, T.kg, 0, True, True, ["bk", "kg0"], ["kb"], "g")
+        fold(kd, T.bk, T.kg, S, True, True, ["bk", "kg1"], ["kd"], "g")
+        if not last:
+            hist = [(T.ip, T.vd[:, :K]), (T.ip, T.vd[:, K:])] + [(T.sh, T.go[:, i * K:(i + 1) * K]) for i in range(2 * t)]
+            mm([(pav, B[:], x_, i == 0, False) for i, (B, x_) in enumerate(hist)], ["ip", "sh", "vh", "vl"], ["pav"], ["v"])
+        fold(ke, T.bk, T.kg, 2 * S, True, True, ["bk", "kg2", "kg3"], ["ke"], "g")
+        gv, gb = T.go[:, 2 * ck:2 * ck + K], T.go[:, 2 * ck + K:2 * ck + 2 * K]
+        gn, hn = "gv%d" % t, "gb%d" % t
+        tt(sm(6), kb, sm(3), A.is_lt, ["kb", "ke", "s3"], ["s6"], ["g"])
+        tt(sm(7), kd, sm(3), A.is_lt, ["kd", "s3"], ["s7"], ["g"])
+        tt(sm(8), ke, sm(2), A.max, ["ke", "s2"], ["s8"], ["g"])
+        tt(gv, sm(6), sm(7), A.mult, ["s6", "s7"], [gn])
+        tt(gb, kb, sm(8), A.is_gt, ["kb", "s8"], [hn], ["g"])
+        if not last:
+            mm([(pav, T.sh[:], gv, False, False), (pav, T.sh[:], gb, False, True)], [gn, hn], ["pav"], ["v"])
+        tt(sm(9), gv, sm(4), A.mult, [gn, "s4"], ["s9"])
+        tt(sm(10), gb, sm(5), A.mult, [hn, "s5"], ["s10"])
+        tt(sm(11), sm(9), nb, A.add, ["s9", "nb%d" % t], ["s11"])
+        u = t + 1
+        if not last:
+            avo = T.av[:, u * N * K + q * K:u * N * K + (q + 1) * K]
+            cp(avo, pav, ["pav"], ["avo%d" % u], ["v"])
+            allsend("a", u, [(avo, avo)], ["avo%d" % u])
+        new = T.nb[:, u * K:(u + 1) * K]
+        tt(new, sm(11), sm(10), A.add, ["s11", "s10"], ["nb%d" % u])
+        if last:
+            break
+        link_msg(u)
+        link_table(u)
+        two_send("m", u, *mpair(u), T.md, ["mh", "ml"])
+        two_table("m", u, *mpair(u), T.md, ["mh", "ml"], T.kt, 1, "dm", ["ktm"])
+        tab_v(*todo[t][2], "b")
+        tabs = ["xt%d_%d" % (n, p) for n in range(u + 1) for p in range(N)]
+        act(T.xc[:, q * S:(q + 1) * S], T.xt[:, :(u + 1) * W].indirect(avo), F.Copy, tabs + ["avo%d" % u], ["xc_own"])
+        cp(T.bn[:], new, ["nb%d" % u], ["bn"])
+        place(new, K, T.ko[:, :K], ["nb%d" % u], ["ko0"], K, 0)
+        cp(T.xv[:], T.xc[:, q * S:(q + 1) * S], ["xc_own"], ["xv"])
+
+    dmas("out", [(T.ylink[:], T.nb[:, RO * K:], ["nb%d" % RO])], ["y"])
+    wait("G", [(k, cnt[k]) for k in ("ls", "V", "S", "P", "G", "out")])

@@ -11,11 +11,11 @@ def _sb(dtype, **kw):
 
 
 SCRATCH = {
-    **_sb("bfloat16", xraw=S, uraw=S, xt=RO * W, ut=W, xc=W, xv=S, lt=LW, kt=W, sg=2 * S, lg=S, kg=3 * S, yb=S, yc=S, xd=S,
+    **_sb("bfloat16", xraw=S, uraw=S, xt=RO * W, ut=S, xc=W, xv=S, lt=LW, kt=W, sg=S, lg=S, kg=3 * S, yb=S, yc=S, xd=S,
           p1=S, c1=S, p2=S, c2=S, p3=S, c3=S, p4=S, c4=S, vd=2 * K, bp=144, bm=144, bl=144, bk=144, ip=128, im=128, sh=128,
           mh=RO * K, ml=RO * K, lm=RO * 2 * K, dm=RO * 2 * K, km=RO * K, go=RO * 2 * K),
-    **_sb("int32", li=K, ci=RO * K, rowi=128, rowj=128, pi=8, t1=RO * K, t2=RO * K),
-    **_sb("float32", row=144, vk=K, vf=K, pf=32, cf=RO * K, mf=RO * K, t3=RO * K, t4=RO * K, t5=RO * K, t6=RO * K,
+    **_sb("int32", li=K, ci=RO * K, rowi=128, rowj=128, pi=8, t1=2 * K, t2=2 * K),
+    **_sb("float32", row=144, vk=K, vf=K, pf=32, cf=RO * K, mf=RO * K, t3=2 * K, t4=2 * K, t5=2 * K, t6=2 * K,
           nb=(RO + 1) * K, de=2 * K, s=12 * K),
     **_sb("uint16", cn=RO * K, cp=RO * K, bn=K, dn=K, ko=3 * K, av=RO * N * K),
     "ld": ("dram", [RO * N, 128, 2 * K], "bfloat16"), "dd": ("dram", [RO * N * 2, 128, K], "bfloat16"),
@@ -24,25 +24,48 @@ SCRATCH = {
     "pg": ("psum", [128, 512], "float32"), "pv": ("psum", [128, 512], "float32"),
 }
 SEMAPHORES = (["V", "S", "P", "G", "ls", "ldl", "ldc", "ldx0", "ldx1", "ldu", "dl", "dd", "dm", "dk", "out",
-               "xs0", "xs1", "xf0", "xf1", "xw0", "xw1", "us", "uf", "uw"]
-              + ["%s%d_%d" % (k, t, q) for k in "almdk" for t in range(RO) for q in range(N)])
+               "xs0", "xs1", "xf0", "xf1", "xw0", "xw1"] + ["h%d" % n for n in range(1, RO)]
+              + ["%s%d_%d" % (k, t, q) for k in "almdkb" for t in range(RO) for q in range(N) if t or k not in "ab"])
 
 
 def rank_program(g, core, T, topo):
-    q = T.rank_of(core)
-    if q is None:
-        return
     cores = T.cores
     same = lambda a, b: topo.host(a) == topo.host(b) and topo.chip(a) == topo.chip(b)
-    sib = [r for r in range(N) if r != q and same(cores[r], core)][0]
-    far = [r for r in range(N) if not same(cores[r], core)]
-    f0 = [r for r in far if topo.die(cores[r]) == topo.die(core)][0]
-    f1 = [r for r in far if r != f0][0]
+    msk = lambda es: sum(1 << e for e in es)
+    dstc = lambda c: DstId(rid=topo.addr(c, core)[0], pnc=topo.addr(c, core)[1])
+    blk = lambda buf, n, p: buf[:, n * W + p * S:n * W + (p + 1) * S]
+
+    def mates_of(r):
+        c = cores[r]
+        far = [p for p in range(N) if not same(cores[p], c)]
+        f = [p for p in far if topo.die(cores[p]) == topo.die(c)][0]
+        return [p for p in range(N) if p != r and same(cores[p], c)][0], f, [p for p in far if p != f][0]
+
+    def helper(r):
+        c = cores[mates_of(r)[1]]
+        return [h for h in topo.cores_of(c) if h not in cores and topo.die(h) == topo.die(c) and topo.may_write(cores[r], h)][0]
+
+    q = T.rank_of(core)
+    if q is None:
+        for r in range(N):
+            if helper(r) == core:
+                tot = 0
+                for n in range(1, RO):
+                    g.wait_ge(T.sem["h%d" % n], len(topo.engines(cores[r], core)))
+                    a, trs = blk(T.xt, n, r), []
+                    for i, p in enumerate(mates_of(r)[1:]):
+                        es = topo.engines(core, cores[p])
+                        es = es[i * len(es) // 2:(i + 1) * len(es) // 2]
+                        tot += len(es)
+                        trs.append(RemoteDMATransfer(dst_ids=[dstc(cores[p])], dma_engine_mask=msk(es),
+                                                     remote_sem=T.sem["b%d_%d" % (n, r)], src=a, dst=a))
+                    g.remote_dma_fused(trs, local_sem=T.sem.ls)
+                g.wait_ge(T.sem.ls, tot)
+        return
+    sib, f0, f1 = mates_of(q)
     peers = [sib, f0, f1]
     fe = topo.engines(core, cores[f0])
     se = [e for e in topo.engines(core, cores[sib]) if e not in fe]
-    msk = lambda es: sum(1 << e for e in es)
-    dst = lambda r: DstId(rid=topo.addr(cores[r], core)[0], pnc=topo.addr(cores[r], core)[1])
 
     Q = {"V": g.vector, "S": g.scalar, "P": g.tensor, "G": g, "Y": g.sync}
     cnt = {}
@@ -123,8 +146,8 @@ def rank_program(g, core, T, topo):
 
     def send(trs, r):
         wait("G", deps("G", r, []))
-        g.remote_dma_fused([RemoteDMATransfer(dst_ids=[dst(p)], dma_engine_mask=msk(es), remote_sem=T.sem[sm], src=a, dst=b)
-                            for p, es, sm, a, b in trs], local_sem=T.sem.ls)
+        g.remote_dma_fused([RemoteDMATransfer(dst_ids=[dstc(c)], dma_engine_mask=msk(es), remote_sem=T.sem[sm], src=a, dst=b)
+                            for c, es, sm, a, b in trs], local_sem=T.sem.ls)
         cnt["ls"] = cnt.get("ls", 0) + sum(len(x[1]) for x in trs)
 
     hf = len(fe) // 2
@@ -135,7 +158,7 @@ def rank_program(g, core, T, topo):
         for p in peers:
             n = len(share[p]) // len(pairs)
             for i, (a, b) in enumerate(pairs):
-                trs.append((p, share[p][i * n:(i + 1) * n], "%s%d_%d" % (kind, t, q), a, b))
+                trs.append((cores[p], share[p][i * n:(i + 1) * n], "%s%d_%d" % (kind, t, q), a, b))
         send(trs, r)
         for p in peers:
             nm = "%s%d_%d" % (kind, t, p)
@@ -148,30 +171,35 @@ def rank_program(g, core, T, topo):
         ts(T.t4[:, :n], T.t1[:, :n], float(1 - 16 * mul), None, A.mult, None, ["t1"], ["t4"])
         ts(T.t5[:, :n], T.t2[:, :n], float(16 * mul - K), None, A.mult, None, ["t2"], ["t5"])
         tt(T.t6[:, :n], T.t3[:, :n], T.t4[:, :n], A.add, ["t3", "t4"], ["t6"])
-        tt(T.t3[:, :n], T.t6[:, :n], T.t5[:, :n], A.add, ["t6", "t5"], ["t3"])
-        cp(out, T.t3[:, :n], ["t3"], wres)
+        tt(T.t4[:, :n], T.t6[:, :n], T.t5[:, :n], A.add, ["t6", "t5"], ["t4"])
+        cp(out, T.t4[:, :n], ["t4"], wres)
 
-    blk = lambda buf, n, p: buf[:, n * W + p * S:n * W + (p + 1) * S]
     PS = {"a": T.pa, "b": T.pb}
     banks3 = lambda z: [z + "0", z + "1", z + "2"]
-    so = {"a": 0, "b": S}
 
-    def tab_pe(n, p, z, minus=None):
+    def tab_pe(n, z, minus):
         it = []
         for a, b in CH:
-            o = n * W - W + p * S
+            o = n * W - W + q * S
             it.append((PS[z][:, a:b], T.ip[:], T.xt[:, o + a:o + b], True, False))
-            it.append((PS[z][:, a:b], T.ip[:], T.ut[:, p * S + a:p * S + b], False, minus is None))
+            it.append((PS[z][:, a:b], T.ip[:], T.ut[:, a:b], False, not minus))
             if minus:
-                it.append((PS[z][:, a:b], T.im[:], T.sg[:, so[minus] + a:so[minus] + b], False, True))
-        mm(it, ["ip", "xt%d_%d" % (n - 1, p), "ut%d" % p] + (["im", "sg" + minus] if minus else []), ["ps" + z], banks3(z))
+                it.append((PS[z][:, a:b], T.im[:], T.sg[:, a:b], False, True))
+        mm(it, ["ip", "xt%d_%d" % (n - 1, q), "ut"] + (["im", "sg"] if minus else []), ["ps" + z], banks3(z))
 
-    def tab_s(z):
-        act(T.sg[:, so[z]:so[z] + S], PS[z][:, :S], F.Sign, ["ps" + z], ["sg" + z], banks3(z), bias=T.pf[:, 28:29])
+    def tab_sign(n):
+        tab_pe(n, "a", False)
+        act(T.sg[:], T.pa[:, :S], F.Sign, ["psa"], ["sg"], banks3("a"), bias=T.pf[:, 28:29])
+        tab_pe(n, "b", True)
 
-    def tab_v(n, p, z):
-        tt(blk(T.xt, n, p), PS[z][:, :S], T.sg[:, so[z]:so[z] + S], A.subtract, ["ps" + z, "sg" + z],
-           ["xt%d_%d" % (n, p)], banks3(z))
+    def tab_end(n):
+        act(blk(T.xt, n, q), T.pb[:, :S], F.Copy, ["psb"], ["xt%d_%d" % (n, q)], banks3("b"))
+
+    def tab_send(n):
+        a = blk(T.xt, n, q)
+        send([(cores[sib], se, "b%d_%d" % (n, q), a, a), (helper(q), fe, "h%d" % n, a, a)], ["xt%d_%d" % (n, q)])
+        for p in peers:
+            wr["xt%d_%d" % (n, p)] = [("b%d_%d" % (n, p), len(se) if p == sib else len(topo.engines(helper(p), core)) // 2)]
 
     def link_msg(t):
         nb = T.nb[:, t * K:(t + 1) * K]
@@ -201,18 +229,33 @@ def rank_program(g, core, T, topo):
                 it.append((tab[h0 + h::16, p * S:(p + 1) * S], src, r0 if p == q else ["%s%d_%d" % (kind, t, p)]))
         dmas(sem, it, w)
 
-    mpair = lambda t: (T.mh[:, t * K:(t + 1) * K], T.ml[:, t * K:(t + 1) * K])
-    sm = lambda i: T.s[:, i * K:(i + 1) * K]
-    pd, pe_, kb, kd, ke = [T.pg[:, i * K:(i + 1) * K] for i in range(5)]
-    pgn, pav = T.pv[:, :K], T.pv[:, K:2 * K]
+    col = lambda buf, t: buf[:, t * K:(t + 1) * K]
+    sm = lambda i: col(T.s, i)
+    pd, pe_, kb, kd = [col(T.pg, i) for i in range(4)]
+    ke, pgn, pav = T.pa[:, :K], T.pv[:, :K], T.pv[:, K:2 * K]
     one = T.pf[:, 20:21]
 
-    def link_lookup(t):
-        act(T.lg[:], T.lt[:, :].indirect(T.cp[:, t * K:(t + 1) * K]), F.Copy, ["lt", "cp0" if t == 0 else "cp"], ["lg"])
-        fold(pd, T.bl, T.lg, 0, True, True, ["bl", "lg"], ["pd"], "g")
+    def m_make(t):
+        tt(col(T.mf, t), col(T.cf, t), T.vf[:], A.min, ["cf", "vf"], ["mf%d" % t])
+        cp(col(T.mh, t), col(T.mf, t), ["mf%d" % t], ["mh%d" % t])
+        tt(col(T.ml, t), col(T.mf, t), col(T.mh, t), A.subtract, ["mf%d" % t, "mh%d" % t], ["ml%d" % t])
 
-    def d_rest(t):
-        hi, lo = T.dm[:, 2 * t * K:(2 * t + 1) * K], T.dm[:, (2 * t + 1) * K:(2 * t + 2) * K]
+    def m_send(t):
+        two_send("m", t, col(T.mh, t), col(T.ml, t), T.md, ["mh%d" % t, "ml%d" % t])
+
+    def m_table(t):
+        two_table("m", t, col(T.mh, t), col(T.ml, t), T.md, ["mh%d" % t, "ml%d" % t], T.kt, 1, "dm", ["ktm"])
+
+    def c_place(t):
+        place(col(T.cf, t), K, col(T.cp, t), ["cf"], ["cp%d" % t], 2 * K, K)
+
+    def link_gather(t):
+        act(T.lg[:], T.lt[:, :].indirect(col(T.cp, t)), F.Copy, ["lt", "cp%d" % t], ["lg"])
+
+    def d_use(t):
+        hi, lo = col(T.dm, 2 * t), col(T.dm, 2 * t + 1)
+        fold(pd, T.bl, T.lg, 0, True, True, ["bl", "lg"], ["pd"], "g")
+        cp(T.dn[:], pd, ["pd"], ["dn"], ["g"])
         cp(hi, pd, ["pd"], ["dh%d" % t], ["g"])
         cp(T.de[:, :K], pd, ["pd"], ["de0"], ["g"])
         tt(lo, pd, hi, A.subtract, ["pd", "dh%d" % t], ["dlo%d" % t], ["g"])
@@ -220,109 +263,99 @@ def rank_program(g, core, T, topo):
         two_send("d", t, hi, lo, T.dd, r)
         two_table("d", t, hi, lo, T.dd, r, T.lt, 0, "dd", ["lt"])
 
+    def open_e():
+        for z in "ba":
+            mm([(PS[z][:, a:b], T.ip[:], T.xv[:, a:b], True, False) for a, b in CH], ["ip", "xv"], ["ps" + z], banks3(z))
+
     H = S // 2
     dmas("ldl", [(T.li[:], T.link[:], [])], ["li"], "S")
     dmas("ldx0", [(T.xraw[:, :H], T.x[:, :H], [])], ["xr0"])
     dmas("ldx1", [(T.xraw[:, H:], T.x[:, H:], [])], ["xr1"], "S")
-    dmas("ldc", [(T.ci[:], T.cand[:], [])], ["ci"])
     dmas("ldu", [(T.uraw[:], T.u[:], [])], ["ur"])
+    dmas("ldc", [(T.ci[:], T.cand[:], [])], ["ci"])
     op("G", lambda: g.iota(T.pi[:, 0:1], [[0, 1]], 0, 1), [], ["pi0"])
     op("G", lambda: g.iota(T.row[:], [[1, 144]], -15, 0, allow_small_or_imprecise_dtypes=True), [], ["row"])
     op("G", lambda: g.iota(T.rowi[:], [[1, 128]], 16, 0), [], ["rowi"])
     op("G", lambda: g.iota(T.vk[:], [[16, K]], q * S, 0, allow_small_or_imprecise_dtypes=True), [], ["vk"])
+    gfill = lambda p: op("G", lambda: g.iota(blk(T.kt, 0, p), [[0, S]], 0, 0, allow_small_or_imprecise_dtypes=True), [], ["kf"])
+    sfill = lambda p: act(blk(T.kt, 0, p), T.xraw[:], F.Copy, ["xr0", "xr1"], ["ktm"])
 
-    L1 = 4096
-    fill(T.lt[:, :L1], 0.0, ["lt_a"])
+    fill(T.lt[:, :4096], 0.0, ["lt_a"])
     cp(T.nb[:, :K], T.li[:], ["li"], ["nb0"])
     link_msg(0)
     for h in range(2):
         own = T.xt[:, q * S + h * H:q * S + (h + 1) * H]
         act(own, T.xraw[:, h * H:(h + 1) * H], F.Copy, ["xr%d" % h], ["xo%d" % h], scale=1.0 / 16)
-        send([(sib, se, "xs%d" % h, own, own), (f0, fe, "xf%d" % h, own, own)], ["xo%d" % h])
+        send([(cores[sib], se, "xs%d" % h, own, own), (cores[f0], fe, "xf%d" % h, own, own)], ["xo%d" % h])
     wr["xt0_%d" % q] = wr["xo1"]
     wr["xt0_%d" % sib] = [("xs0", len(se)), ("xs1", len(se))]
     wr["xt0_%d" % f0] = [("xf0", len(fe)), ("xf1", len(fe))]
     wr["xt0_%d" % f1] = [("xw0", len(se)), ("xw1", len(se))]
-    fill(T.pf[:, 28:29], -31.0 / 32, ["pfs"])
-    fill(one, 1.0, ["pf1"])
-    uo = blk(T.ut, 0, q)
-    ts(uo, T.uraw[:], 1.0 / 16, -1.0, A.mult, A.add, ["ur"], ["ut%d" % q])
-    send([(sib, se, "us", uo, uo), (f0, fe, "uf", uo, uo)], ["ut%d" % q])
-    wr["ut%d" % sib] = [("us", len(se))]
-    wr["ut%d" % f0] = [("uf", len(fe))]
-    wr["ut%d" % f1] = [("uw", len(se))]
+    gfill(0)
     for h in range(2):
         wait("G", [("xf%d" % h, len(fe))])
         a = T.xt[:, f0 * S + h * H:f0 * S + (h + 1) * H]
-        send([(sib, se, "xw%d" % h, a, a)], [])
-    fill(T.lt[:, L1:], 0.0, ["lt"])
-    link_table(0)
-    for p in range(N):
-        act(T.kt[:, p * S:(p + 1) * S], T.xraw[:], F.Copy, ["xr0", "xr1"], ["ktm", "ktk"])
-    ts(T.pi[:, 4:5], T.pi[:, 0:1], 15, None, A.bitwise_and, None, ["pi0"], ["pi4"])
+        send([(cores[sib], se, "xw%d" % h, a, a)], [])
+    gfill(1)
+    sfill(2)
     cp(T.pf[:, 0:1], T.pi[:, 0:1], ["pi0"], ["p"])
-    cp(T.cf[:], T.ci[:], ["ci"], ["cf"])
-    cp(T.pf[:, 4:5], T.pi[:, 4:5], ["pi4"], ["pm"])
+    ts(T.pi[:, 4:5], T.pi[:, 0:1], 15, None, A.bitwise_and, None, ["pi0"], ["pi4"])
+    fill(T.pf[:, 28:29], -31.0 / 32, ["pfs"])
+    fill(one, 1.0, ["pf1"])
     ts(T.ip[:], T.row[:, 15:143], T.pf[:, 0:1], None, A.is_equal, None, ["row", "p"], ["ip"])
     ts(T.im[:], T.row[:, 15:143], T.pf[:, 0:1], -1.0, A.is_equal, A.mult, ["row", "p"], ["im"])
+    fill(T.lt[:, 4096:6144], 0.0, ["lt_b"])
+    ts(T.ut[:], T.uraw[:], 1.0 / 16, -1.0, A.mult, A.add, ["ur"], ["ut"])
+    fill(T.lt[:, 6144:], 0.0, ["lt"])
+    link_table(0)
+    wait("S", wr["pfs"] + wr["pf1"])
+    tab_sign(1)
+    sfill(3)
+    tab_end(1)
+    tab_send(1)
+    wr["ktm"] = wr["ktm"] + wr["kf"]
+    wr["ktk"] = wr["ktm"]
+    cp(T.cf[:], T.ci[:], ["ci"], ["cf"])
+    cp(T.pf[:, 4:5], T.pi[:, 4:5], ["pi4"], ["pm"])
+    c_place(0)
+    link_gather(0)
     tt(T.pf[:, 8:9], T.pf[:, 0:1], T.pf[:, 4:5], A.subtract, ["p", "pm"], ["g16"])
     ts(T.pf[:, 12:13], T.pf[:, 4:5], 2.0, None, A.is_lt, None, ["pm"], ["wl"])
-    place(T.cf[:, :K], K, T.cp[:, :K], ["cf"], ["cp0"], 2 * K, K)
-    ts(T.bl[:], T.row[:], T.pf[:, 8:9], T.pf[:, 12:13], A.is_equal, A.mult, ["row", "g16", "wl"], ["bl"])
-    wait("S", wr["pfs"] + wr["pf1"])
-    tab_pe(1, q, "b")
-    tab_s("b")
-    link_lookup(0)
-    ts(T.pf[:, 13:14], T.pf[:, 4:5], 0.0, 16385.0, A.is_equal, A.mult, ["pm"], ["wk0"])
-    ts(T.pf[:, 14:15], T.pf[:, 4:5], 3.0, None, A.is_lt, None, ["pm"], ["wk1"])
     ts(T.vf[:], T.vk[:], T.pf[:, 4:5], None, A.add, None, ["vk", "pm"], ["vf"])
-    ts(T.rowj[:], T.rowi[:], 127, None, A.bitwise_and, None, ["rowi"], ["rowj"])
-    tt(T.pf[:, 16:17], T.pf[:, 13:14], T.pf[:, 14:15], A.subtract, ["wk0", "wk1"], ["wk"])
-    for t in range(RO):
-        tt(T.mf[:, t * K:(t + 1) * K], T.cf[:, t * K:(t + 1) * K], T.vf[:], A.min, ["cf", "vf"], ["mf"])
-    tab_v(1, q, "b")
-    cp(T.mh[:], T.mf[:], ["mf"], ["mh"])
-    cp(T.cn[:], T.ci[:], ["ci"], ["cn"])
-    tt(T.ml[:], T.mf[:], T.mh[:], A.subtract, ["mf", "mh"], ["ml"])
-    two_send("m", 0, *mpair(0), T.md, ["mh", "ml"])
-    two_table("m", 0, *mpair(0), T.md, ["mh", "ml"], T.kt, 1, "dm", ["ktm"])
-    tab_pe(2, q, "a")
-    tab_s("a")
-    tab_pe(2, q, "b", "a")
-    act(blk(T.xt, 2, q), T.pb[:, :S], F.Copy, ["psb"], ["xt2_%d" % q], banks3("b"))
-    cp(T.bn[:], T.li[:], ["li"], ["bn"])
+    ts(T.bl[:], T.row[:], T.pf[:, 8:9], T.pf[:, 12:13], A.is_equal, A.mult, ["row", "g16", "wl"], ["bl"])
     ts(T.xv[:], T.xraw[:], 1.0 / 16, None, A.mult, None, ["xr0", "xr1"], ["xv"])
+    open_e()
+    m_make(0)
+    m_send(0)
+    m_table(0)
+    cp(T.bn[:], T.li[:], ["li"], ["bn"])
+    cp(T.cn[:], T.ci[:], ["ci"], ["cn"])
     ts(T.bp[:], T.row[:], T.pf[:, 8:9], 16.0, A.is_equal, A.mult, ["row", "g16"], ["bp"])
     ts(T.bm[:], T.row[:], T.pf[:, 8:9], -16.0, A.is_equal, A.mult, ["row", "g16"], ["bm"])
-    ts(T.bk[:], T.row[:], T.pf[:, 8:9], T.pf[:, 16:17], A.is_equal, A.mult, ["row", "g16", "wk"], ["bk"])
-    ts(T.sh[:], T.rowj[:], T.pf[:, 0:1], float(W), A.is_equal, A.mult, ["rowj", "p"], ["sh"])
-    cp(T.vd[:, :K], T.vf[:], ["vf"], ["vh"])
-    cp(T.dn[:], pd, ["pd"], ["dn"], ["g"])
-    d_rest(0)
-    tt(T.vd[:, K:], T.vf[:], T.vd[:, :K], A.subtract, ["vf", "vh"], ["vl"])
     place(T.nb[:, :K], K, T.ko[:, :K], ["nb0"], ["ko0"], K, 0)
-    place(T.cf[:, K:], (RO - 1) * K, T.cp[:, K:], ["cf"], ["cp"], 2 * K, K)
-    tab_pe(1, sib, "a")
-    tab_s("a")
-    tab_pe(3, q, "b")
-    tab_s("b")
-    tab_v(1, sib, "a")
-    tab_v(3, q, "b")
-    wait("G", [("uf", len(fe))])
-    a = blk(T.ut, 0, f0)
-    send([(sib, se, "uw", a, a)], [])
-    todo = [[(1, f0), (1, f1), (2, sib)], [(2, f0), (2, f1), (3, sib)], [(3, f0), (3, f1), (4, q)], [(4, sib), (4, f0), (4, f1)]]
+    d_use(0)
+
+    def late_start():
+        ts(T.pf[:, 13:14], T.pf[:, 4:5], 0.0, 16385.0, A.is_equal, A.mult, ["pm"], ["wk0"])
+        ts(T.pf[:, 14:15], T.pf[:, 4:5], 3.0, None, A.is_lt, None, ["pm"], ["wk1"])
+        ts(T.rowj[:], T.rowi[:], 127, None, A.bitwise_and, None, ["rowi"], ["rowj"])
+        cp(T.vd[:, :K], T.vf[:], ["vf"], ["vh"])
+        tt(T.pf[:, 16:17], T.pf[:, 13:14], T.pf[:, 14:15], A.subtract, ["wk0", "wk1"], ["wk"])
+        ts(T.sh[:], T.rowj[:], T.pf[:, 0:1], float(W), A.is_equal, A.mult, ["rowj", "p"], ["sh"])
+        tt(T.vd[:, K:], T.vf[:], T.vd[:, :K], A.subtract, ["vf", "vh"], ["vl"])
+        ts(T.bk[:], T.row[:], T.pf[:, 8:9], T.pf[:, 16:17], A.is_equal, A.mult, ["row", "g16", "wk"], ["bk"])
 
     for t in range(RO):
-        nb = T.nb[:, t * K:(t + 1) * K]
+        nb = col(T.nb, t)
         last = t == RO - 1
+        u = t + 1
         if t == 0:
             X, xr = T.xt, ["xt0_%d" % p for p in range(N)]
         else:
             X, xr = T.xc, ["xc_own", "xc_V", "xc_S"]
             cols = [c for p in range(N) if p != q for c in range(p * K, (p + 1) * K)]
             tabs = ["xt%d_%d" % (n, p) for n in range(t + 1) for p in range(N)]
-            for e, part in (("V", cols[:len(cols) // 2]), ("S", cols[len(cols) // 2:])):
+            for e, part in (("V", cols[:112]), ("S", cols[112:])):
                 runs = []
                 for c in part:
                     if runs and runs[-1][1] == c:
@@ -336,127 +369,119 @@ def rank_program(g, core, T, topo):
                         cp(T.xc[:, 16 * a:16 * b], src, r, ["xc_V"])
                     else:
                         act(T.xc[:, 16 * a:16 * b], src, F.Copy, r, ["xc_S"])
-            link_lookup(t)
+            link_gather(t)
         win = X[:, :W]
-        tt(T.yb[:], win.indirect(T.bn[:]), T.xv[:], A.subtract, xr + ["bn", "xv"], ["yb"])
+        term = lambda z, y, yr: mm([(PS[z][:, a:b], T.ip[:], y[:, a:b], False, False) for a, b in CH], ["ip", yr], ["ps" + z], banks3(z))
+        xdt = lambda z, i: mm([(PS[z][:, CH[i][0]:CH[i][1]], T.im[:], T.xd[:, CH[i][0]:CH[i][1]], False, True)],
+                              ["im", "xd%d" % i], ["e%s%d" % (z, i)], [z + str(i)])
+        gf = lambda B, src, r, first=False, end=False: fold(pgn, B, src, 0, first, end, ["bp", "bm"] + r, ["pgn"], "v")
         ck = t * K
-        if t == 0:
-            tt(T.yc[:], win.indirect(T.cn[:, ck:ck + K]), T.xv[:], A.subtract, xr + ["cn", "xv"], ["yc"])
-        else:
-            tt(T.yc[:, :H], win.indirect(T.cn[:, ck:ck + K // 2]), T.xv[:, :H], A.subtract, xr + ["cn", "xv"], ["yc"])
-            act(T.p1[:], T.yb[:], F.Relu, ["yb"], ["p1"], bias=one)
-            cp(T.dn[:], pd, ["pd"], ["dn"], ["g"])
-            tt(T.yc[:, H:], win.indirect(T.cn[:, ck + K // 2:ck + K]), T.xv[:, H:], A.subtract, xr + ["cn", "xv"], ["yc"])
+        tt(T.yb[:], win.indirect(T.bn[:]), T.xv[:], A.subtract, xr + ["bn", "xv"], ["yb"])
+        term("b", T.yb, "yb")
+        ts(T.p1[:], T.yb[:], -1.0, None, A.max, None, ["yb"], ["p1"])
+        gf(T.bm, T.p1, ["p1"], True)
+        ts(T.c1[:], T.yb[:], 0.0, 1.0, A.max, A.min, ["yb"], ["c1"])
+        tt(T.yc[:, :H], win.indirect(T.cn[:, ck:ck + K // 2]), T.xv[:, :H], A.subtract, xr + ["cn", "xv"], ["yc"])
+        if t > 0:
+            d_use(t)
+        gf(T.bp, T.c1, ["c1"])
+        tt(T.yc[:, H:], win.indirect(T.cn[:, ck + K // 2:ck + K]), T.xv[:, H:], A.subtract, xr + ["cn", "xv"], ["yc"])
         for i, (a, b) in enumerate(CH):
             act(T.xd[:, a:b], win.indirect(T.dn[:, a // 16:b // 16]), F.Copy, xr + ["dn"], ["xd%d" % i])
-        if t == 0:
-            act(T.p1[:], T.yb[:], F.Relu, ["yb"], ["p1"], bias=one)
-        else:
-            d_rest(t)
-        for z, y, yr in (("b", T.yb, "yb"), ("a", T.yc, "yc")):
-            it = []
-            for a, b in CH:
-                it.append((PS[z][:, a:b], T.ip[:], T.xv[:, a:b], True, False))
-                it.append((PS[z][:, a:b], T.ip[:], y[:, a:b], False, False))
-            mm(it, ["ip", yr, "xv"], ["ps" + z], banks3(z))
-            if z == "b" and t > 0:
-                fold(pgn, T.bm, T.p1, 0, True, False, ["bm", "p1"], ["pgn"], "v")
         ts(T.p3[:], T.yc[:], -1.0, None, A.max, None, ["yc"], ["p3"])
         ts(T.c3[:], T.yc[:], 0.0, 1.0, A.max, A.min, ["yc"], ["c3"])
-        ts(T.c1[:], T.p1[:], 1.0, 2.0, A.max, A.min, ["p1"], ["c1"])
-        for i, (a, b) in enumerate(CH):
-            for z in "ba":
-                mm([(PS[z][:, a:b], T.im[:], T.xd[:, a:b], False, True)], ["im", "xd%d" % i], ["e%s%d" % (z, i)], [z + str(i)])
-            if i == 0:
-                fold(pgn, T.bp, T.p3, 0, t == 0, False, ["bp", "p3"], ["pgn"], "v")
-            if i == 1:
-                fold(pgn, T.bm, T.c3, 0, False, False, ["bm", "c3"], ["pgn"], "v")
-        if t == 0:
-            fold(pgn, T.bm, T.p1, 0, False, False, ["bm", "p1"], ["pgn"], "v")
-        fold(pgn, T.bp, T.c1, 0, False, False, ["bp", "c1"], ["pgn"], "v")
-        a, b = CH[0]
-        ts(T.p4[:, a:b], T.pb[:, a:b], -1.0, None, A.max, None, ["eb0"], ["p4_0"], ["b0"])
-        ts(T.c4[:, a:b], T.p4[:, a:b], 0.0, 1.0, A.max, A.min, ["p4_0"], ["c4_0"])
-        for z, i in (("b", 1), ("b", 2), ("a", 0), ("a", 1), ("a", 2)):
+        xdt("b", 0)
+        term("a", T.yc, "yc")
+        xdt("b", 1)
+        xdt("b", 2)
+        gf(T.bp, T.p3, ["p3"])
+        for i in range(3):
+            xdt("a", i)
+        gf(T.bm, T.c3, ["c3"])
+        for z, i in (("b", 0), ("b", 1), ("b", 2), ("a", 0), ("a", 1), ("a", 2)):
             a, b = CH[i]
             pz, cz, nm = (T.p4, T.c4, "4_%d" % i) if z == "b" else (T.p2, T.c2, "2_%d" % i)
             act(pz[:, a:b], PS[z][:, a:b], F.Relu, ["e%s%d" % (z, i)], ["p" + nm], [z + str(i)], bias=one)
-            ts(cz[:, a:b], pz[:, a:b], 1.0, 2.0, A.max, A.min, ["p" + nm], ["c" + nm])
-            if (z, i) == ("b", 2):
-                fold(pgn, T.bp, T.p4, 0, False, False, ["bp", "p4_0", "p4_1", "p4_2"], ["pgn"], "v")
-                fold(pgn, T.bm, T.c4, 0, False, False, ["bm", "c4_0", "c4_1", "c4_2"], ["pgn"], "v")
-        fold(pgn, T.bm, T.p2, 0, False, False, ["bm", "p2_0", "p2_1", "p2_2"], ["pgn"], "v")
-        fold(pgn, T.bp, T.c2, 0, False, True, ["bp", "c2_0", "c2_1", "c2_2"], ["pgn"], "v")
-        km = T.km[:, ck:ck + K]
+            if i == 1:
+                ts(cz[:, :b], pz[:, :b], 1.0, 2.0, A.max, A.min, ["p" + nm], ["c" + nm])
+            if i == 2:
+                ts(cz[:, a:b], pz[:, a:b], 1.0, 2.0, A.max, A.min, ["p" + nm], ["c" + nm])
+                w_ = (T.bp, T.bm) if z == "b" else (T.bm, T.bp)
+                gf(w_[0], pz, ["p" + nm])
+                gf(w_[1], cz, ["c" + nm], False, z == "a")
+        km = col(T.km, t)
+        if not last:
+            m_make(u)
         ts(km, pgn, 0.0, None, A.max, None, ["pgn"], ["km%d" % t], ["v"])
         allsend("k", t, [(km, T.kd[t * N + q])], ["km%d" % t])
         dmas("dk", [(T.kt[0::16, p * S:(p + 1) * S], km if p == q else T.kd[t * N + p],
                      ["km%d" % t] if p == q else ["k%d_%d" % (t, p)]) for p in [q] + peers], ["ktk"])
+        if not last:
+            wait("G", wr["ktk"])
+            m_send(u)
         act(T.lg[:], T.lt[:, :W].indirect(T.ko[:, :K]), F.Copy, ["lt", "ko0"], ["lg"])
-        if not last:
-            tab_pe(*todo[t][0], "b")
         fold(pe_, T.bl, T.lg, 0, True, True, ["bl", "lg"], ["pe"], "g")
-        if not last:
-            tab_pe(*todo[t][1], "a")
-            tab_s("b")
-            tab_s("a")
+        if t + 2 < RO:
+            tab_sign(t + 2)
         ts(sm(11), km, 16384.0, None, A.mult, None, ["km%d" % t], ["s11"])
         ts(sm(1), km, 32768.0, -6000.0, A.mult, A.add, ["km%d" % t], ["s1"])
-        tt(sm(4), T.cf[:, ck:ck + K], nb, A.subtract, ["cf", "nb%d" % t], ["s4"])
-        tt(sm(0), sm(11), T.mf[:, ck:ck + K], A.subtract, ["s11", "mf"], ["s0"])
+        tt(sm(4), col(T.cf, t), nb, A.subtract, ["cf", "nb%d" % t], ["s4"])
+        tt(sm(0), sm(11), col(T.mf, t), A.subtract, ["s11", "mf%d" % t], ["s0"])
         cp(T.de[:, K:], pe_, ["pe"], ["de1"], ["g"])
         ts(sm(2), sm(0), 0.0, None, A.max, None, ["s0"], ["s2"])
+        place(T.de[:], 2 * K, T.ko[:, K:], ["de0", "de1"], ["ko1"], K, 0)
         tt(sm(3), sm(0), sm(1), A.min, ["s0", "s1"], ["s3"])
         tt(sm(5), T.de[:, K:], nb, A.subtract, ["de1", "nb%d" % t], ["s5"])
-        place(T.de[:], 2 * K, T.ko[:, K:], ["de0", "de1"], ["ko1"], K, 0)
+        if t == 0:
+            late_start()
         if not last:
-            tab_v(*todo[t][0], "b")
-            tab_pe(*todo[t][2], "b")
-            tab_v(*todo[t][1], "a")
-            tab_s("b")
+            c_place(u)
         kr = ["ktm", "ktk", "ko0", "ko1"]
         kw = T.kt[:, :]
         cp(T.kg[:, :S], kw.indirect(T.ko[:, :K]), kr, ["kg0"])
         act(T.kg[:, S:2 * S], kw.indirect(T.ko[:, K:2 * K]), F.Copy, kr, ["kg1"])
         cp(T.kg[:, 2 * S:2 * S + H], kw.indirect(T.ko[:, 2 * K:2 * K + K // 2]), kr, ["kg2"])
         act(T.kg[:, 2 * S + H:], kw.indirect(T.ko[:, 2 * K + K // 2:]), F.Copy, kr, ["kg3"])
+        if t + 2 < RO:
+            tab_end(t + 2)
+        if not last:
+            hist = [(T.ip, T.vd[:, :K]), (T.ip, T.vd[:, K:])] + [(T.sh, col(T.go, i)) for i in range(2 * t)]
+            mm([(pav, B[:], x_, i == 0, False) for i, (B, x_) in enumerate(hist)], ["ip", "sh", "vh", "vl"], ["pav"], ["v"])
         fold(kb, T.bk, T.kg, 0, True, True, ["bk", "kg0"], ["kb"], "g")
         fold(kd, T.bk, T.kg, S, True, True, ["bk", "kg1"], ["kd"], "g")
-        if not last:
-            hist = [(T.ip, T.vd[:, :K]), (T.ip, T.vd[:, K:])] + [(T.sh, T.go[:, i * K:(i + 1) * K]) for i in range(2 * t)]
-            mm([(pav, B[:], x_, i == 0, False) for i, (B, x_) in enumerate(hist)], ["ip", "sh", "vh", "vl"], ["pav"], ["v"])
-        fold(ke, T.bk, T.kg, 2 * S, True, True, ["bk", "kg2", "kg3"], ["ke"], "g")
-        gv, gb = T.go[:, 2 * ck:2 * ck + K], T.go[:, 2 * ck + K:2 * ck + 2 * K]
+        fold(ke, T.bk, T.kg, 2 * S, True, True, ["bk", "kg2", "kg3"], ["ke"], "a0")
+        gv, gb = col(T.go, 2 * t), col(T.go, 2 * t + 1)
         gn, hn = "gv%d" % t, "gb%d" % t
-        tt(sm(6), kb, sm(3), A.is_lt, ["kb", "ke", "s3"], ["s6"], ["g"])
+        tt(sm(6), kb, sm(3), A.is_lt, ["kb", "s3"], ["s6"], ["g"])
         tt(sm(7), kd, sm(3), A.is_lt, ["kd", "s3"], ["s7"], ["g"])
-        tt(sm(8), ke, sm(2), A.max, ["ke", "s2"], ["s8"], ["g"])
         tt(gv, sm(6), sm(7), A.mult, ["s6", "s7"], [gn])
+        tt(sm(9), gv, sm(4), A.mult, [gn, "s4"], ["s9"])
+        tt(sm(8), ke, sm(2), A.max, ["ke", "s2"], ["s8"], ["a0"])
+        tt(sm(11), sm(9), nb, A.add, ["s9", "nb%d" % t], ["s11"])
         tt(gb, kb, sm(8), A.is_gt, ["kb", "s8"], [hn], ["g"])
         if not last:
             mm([(pav, T.sh[:], gv, False, False), (pav, T.sh[:], gb, False, True)], [gn, hn], ["pav"], ["v"])
-        tt(sm(9), gv, sm(4), A.mult, [gn, "s4"], ["s9"])
         tt(sm(10), gb, sm(5), A.mult, [hn, "s5"], ["s10"])
-        tt(sm(11), sm(9), nb, A.add, ["s9", "nb%d" % t], ["s11"])
-        u = t + 1
         if not last:
             avo = T.av[:, u * N * K + q * K:u * N * K + (q + 1) * K]
             cp(avo, pav, ["pav"], ["avo%d" % u], ["v"])
             allsend("a", u, [(avo, avo)], ["avo%d" % u])
-        new = T.nb[:, u * K:(u + 1) * K]
+        new = col(T.nb, u)
         tt(new, sm(11), sm(10), A.add, ["s11", "s10"], ["nb%d" % u])
         if last:
             break
         link_msg(u)
         link_table(u)
-        two_send("m", u, *mpair(u), T.md, ["mh", "ml"])
-        two_table("m", u, *mpair(u), T.md, ["mh", "ml"], T.kt, 1, "dm", ["ktm"])
-        tab_v(*todo[t][2], "b")
+        if u + 1 < RO:
+            wait("G", wr["lt"])
+            tab_send(u + 1)
+        m_table(u)
         tabs = ["xt%d_%d" % (n, p) for n in range(u + 1) for p in range(N)]
         act(T.xc[:, q * S:(q + 1) * S], T.xt[:, :(u + 1) * W].indirect(avo), F.Copy, tabs + ["avo%d" % u], ["xc_own"])
         cp(T.bn[:], new, ["nb%d" % u], ["bn"])
         place(new, K, T.ko[:, :K], ["nb%d" % u], ["ko0"], K, 0)
         cp(T.xv[:], T.xc[:, q * S:(q + 1) * S], ["xc_own"], ["xv"])
+        open_e()
 
     dmas("out", [(T.ylink[:], T.nb[:, RO * K:], ["nb%d" % RO])], ["y"])
     wait("G", [(k, cnt[k]) for k in ("ls", "V", "S", "P", "G", "out")])

from concourse.bass import DstId, RemoteDMATransfer
from concourse.mybir import AluOpType as A, ActivationFunctionType as F

N, S, RO, W, K = 4, 1280, 5, 5120, 80
CH = [(0, 512), (512, 1024), (1024, 1280)]
LW = 2 * W + K


def _sb(dtype, **kw):
    return {k: ("sbuf", [128, n], dtype) for k, n in kw.items()}


SCRATCH = {
    **_sb("bfloat16", xraw=S, uraw=S, xt=RO * W, ut=S, xc=W, xv=S, lt=LW, kt=W, sg=S, lg=S, kg=3 * S, yb=S, yc=S, xd=S,
          p1=S, c1=S, p2=S, c2=S, p3=S, c3=S, p4=S, c4=S, vd=2 * K, bp=144, bm=144, bl=144, bk=144, ip=128, im=128, sh=128,
          mh=RO * K, ml=RO * K, lm=RO * 2 * K, dm=RO * 2 * K, km=RO * K, go=RO * 2 * K),
    **_sb("int32", li=K, ci=RO * K, rowi=128, rowj=128, pi=8, t1=2 * K, t2=2 * K),
    **_sb("float32", row=144, vk=K, vf=K, pf=32, cf=RO * K, mf=RO * K, t3=2 * K, t4=2 * K, t5=2 * K, t6=2 * K,
          nb=(RO + 1) * K, de=2 * K, s=12 * K),
    **_sb("uint16", cn=RO * K, cp=RO * K, bn=K, dn=K, ko=3 * K, av=RO * N * K),
    "ld": ("dram", [RO * N, 128, 2 * K], "bfloat16"), "dd": ("dram", [RO * N * 2, 128, K], "bfloat16"),
    "md": ("dram", [RO * N * 2, 128, K], "bfloat16"), "kd": ("dram", [RO * N, 128, K], "bfloat16"),
    "pa": ("psum", [128, 1536], "float32"), "pb": ("psum", [128, 1536], "float32"),
    "pg": ("psum", [128, 512], "float32"), "pv": ("psum", [128, 512], "float32"),
}
SEMAPHORES = (["V", "S", "P", "G", "ls", "ldl", "ldc", "ldx0", "ldx1", "ldu", "dl", "dd", "dm", "dk", "out",
               "xs0", "xs1", "xf0", "xf1", "xw0", "xw1"] + ["h%d" % n for n in range(1, RO)]
              + ["%s%d_%d" % (k, t, q) for k in "almdkb" for t in range(RO) for q in range(N) if t or k not in "ab"])


def rank_program(g, core, T, topo):
    cores = T.cores
    same = lambda a, b: topo.host(a) == topo.host(b) and topo.chip(a) == topo.chip(b)
    msk = lambda es: sum(1 << e for e in es)
    dstc = lambda c: DstId(rid=topo.addr(c, core)[0], pnc=topo.addr(c, core)[1])
    blk = lambda buf, n, p: buf[:, n * W + p * S:n * W + (p + 1) * S]

    def mates_of(r):
        c = cores[r]
        far = [p for p in range(N) if not same(cores[p], c)]
        f = [p for p in far if topo.die(cores[p]) == topo.die(c)][0]
        return [p for p in range(N) if p != r and same(cores[p], c)][0], f, [p for p in far if p != f][0]

    def helper(r):
        c = cores[mates_of(r)[1]]
        return [h for h in topo.cores_of(c) if h not in cores and topo.die(h) == topo.die(c) and topo.may_write(cores[r], h)][0]

    q = T.rank_of(core)
    if q is None:
        for r in range(N):
            if helper(r) == core:
                tot = 0
                for n in range(1, RO):
                    g.wait_ge(T.sem["h%d" % n], len(topo.engines(cores[r], core)))
                    a, trs = blk(T.xt, n, r), []
                    for i, p in enumerate(mates_of(r)[1:]):
                        es = topo.engines(core, cores[p])
                        es = es[i * len(es) // 2:(i + 1) * len(es) // 2]
                        tot += len(es)
                        trs.append(RemoteDMATransfer(dst_ids=[dstc(cores[p])], dma_engine_mask=msk(es),
                                                     remote_sem=T.sem["b%d_%d" % (n, r)], src=a, dst=a))
                    g.remote_dma_fused(trs, local_sem=T.sem.ls)
                g.wait_ge(T.sem.ls, tot)
        return
    sib, f0, f1 = mates_of(q)
    peers = [sib, f0, f1]
    fe = topo.engines(core, cores[f0])
    se = [e for e in topo.engines(core, cores[sib]) if e not in fe]

    Q = {"V": g.vector, "S": g.scalar, "P": g.tensor, "G": g, "Y": g.sync}
    cnt = {}
    waited = {k: {} for k in Q}
    wr, rd, bank = {}, {}, {}

    def wait(e, toks):
        need = {}
        for s_, v in toks:
            need[s_] = max(need.get(s_, 0), v)
        for s_, v in need.items():
            if waited[e].get(s_, 0) < v:
                Q[e].wait_ge(T.sem[s_], v)
                waited[e][s_] = v

    def deps(e, r, w, banks=()):
        toks = []
        for x in r:
            toks += wr[x]
        for x in w:
            toks += [k for k in wr.get(x, []) if k[0] != e] + rd.get(x, [])
        for b in banks:
            toks += [k for k in bank.get(b, {}).values() if k[0] != e]
        return toks

    def done(tok, r, w, banks=()):
        for x in r:
            rd.setdefault(x, []).append(tok)
        for x in w:
            wr[x] = [tok]
            rd[x] = []
        for b in banks:
            bank.setdefault(b, {})[tok[0]] = tok

    def op(e, fn, r, w, banks=()):
        wait(e, deps(e, r, w, banks))
        cnt[e] = cnt.get(e, 0) + 1
        fn().then_inc(T.sem[e], 1)
        done((e, cnt[e]), r, w, banks)

    def ts(out, in0, s1, s2, o0, o1, r, w, banks=()):
        if s2 is None:
            op("V", lambda: g.vector.tensor_scalar(out, in0, s1, None, o0), r, w, banks)
        else:
            op("V", lambda: g.vector.tensor_scalar(out, in0, s1, s2, o0, o1), r, w, banks)

    def tt(out, a, b, o, r, w, banks=()):
        op("V", lambda: g.vector.tensor_tensor(out, a, b, o), r, w, banks)

    def cp(out, a, r, w, banks=()):
        op("V", lambda: g.vector.tensor_copy(out, a), r, w, banks)

    def fill(out, v, w):
        op("V", lambda: g.vector.memset(out, v), [], w)

    def act(out, a, f, r, w, banks=(), **kw):
        op("S", lambda: g.scalar.activation(out, a, f, **kw), r, w, banks)

    def mm(items, r, w, banks):
        def fn():
            last = None
            for it in items:
                last = g.tensor.matmul(*it)
            return last
        op("P", fn, r, w, banks)

    def fold(out, B, src, c0, first, last, r, w, b):
        mm([(out, B[:, 15 - i:143 - i], src[:, c0 + i:c0 + S:16], first and i == 0, last and i == 15) for i in range(16)],
           r, w, [b])

    def dmas(sem, items, w, e="Y"):
        wait(e, deps(e, [], w))
        for o, i, r in items:
            wait(e, deps(e, r, []))
            Q[e].dma_start(o, i).then_inc(T.sem[sem], 16)
            cnt[sem] = cnt.get(sem, 0) + 16
        done((sem, cnt[sem]), [], w)

    def send(trs, r):
        wait("G", deps("G", r, []))
        g.remote_dma_fused([RemoteDMATransfer(dst_ids=[dstc(c)], dma_engine_mask=msk(es), remote_sem=T.sem[sm], src=a, dst=b)
                            for c, es, sm, a, b in trs], local_sem=T.sem.ls)
        cnt["ls"] = cnt.get("ls", 0) + sum(len(x[1]) for x in trs)

    hf = len(fe) // 2
    share = {sib: se, f0: fe[:hf], f1: fe[hf:]}

    def allsend(kind, t, pairs, r):
        trs = []
        for p in peers:
            n = len(share[p]) // len(pairs)
            for i, (a, b) in enumerate(pairs):
                trs.append((cores[p], share[p][i * n:(i + 1) * n], "%s%d_%d" % (kind, t, q), a, b))
        send(trs, r)
        for p in peers:
            nm = "%s%d_%d" % (kind, t, p)
            wr[nm] = [(nm, len(share[p]))]

    def place(src, n, out, res, wres, mul, base):
        ts(T.t1[:, :n], src, 1.0 / 16, -0.46875, A.mult, A.add, res, ["t1"])
        ts(T.t2[:, :n], src, 1.0 / S, -0.4996, A.mult, A.add, res, ["t2"])
        ts(T.t3[:, :n], src, float(mul), float(base), A.mult, A.add, res, ["t3"])
        ts(T.t4[:, :n], T.t1[:, :n], float(1 - 16 * mul), None, A.mult, None, ["t1"], ["t4"])
        ts(T.t5[:, :n], T.t2[:, :n], float(16 * mul - K), None, A.mult, None, ["t2"], ["t5"])
        tt(T.t6[:, :n], T.t3[:, :n], T.t4[:, :n], A.add, ["t3", "t4"], ["t6"])
        tt(T.t4[:, :n], T.t6[:, :n], T.t5[:, :n], A.add, ["t6", "t5"], ["t4"])
        cp(out, T.t4[:, :n], ["t4"], wres)

    PS = {"a": T.pa, "b": T.pb}
    banks3 = lambda z: [z + "0", z + "1", z + "2"]

    def tab_pe(n, z, minus):
        it = []
        for a, b in CH:
            o = n * W - W + q * S
            it.append((PS[z][:, a:b], T.ip[:], T.xt[:, o + a:o + b], True, False))
            it.append((PS[z][:, a:b], T.ip[:], T.ut[:, a:b], False, not minus))
            if minus:
                it.append((PS[z][:, a:b], T.im[:], T.sg[:, a:b], False, True))
        mm(it, ["ip", "xt%d_%d" % (n - 1, q), "ut"] + (["im", "sg"] if minus else []), ["ps" + z], banks3(z))

    def tab_sign(n):
        tab_pe(n, "a", False)
        act(T.sg[:], T.pa[:, :S], F.Sign, ["psa"], ["sg"], banks3("a"), bias=T.pf[:, 28:29])
        tab_pe(n, "b", True)

    def tab_end(n):
        act(blk(T.xt, n, q), T.pb[:, :S], F.Copy, ["psb"], ["xt%d_%d" % (n, q)], banks3("b"))

    def tab_send(n):
        a = blk(T.xt, n, q)
        send([(cores[sib], se, "b%d_%d" % (n, q), a, a), (helper(q), fe, "h%d" % n, a, a)], ["xt%d_%d" % (n, q)])
        for p in peers:
            wr["xt%d_%d" % (n, p)] = [("b%d_%d" % (n, p), len(se) if p == sib else len(topo.engines(helper(p), core)) // 2)]

    def link_msg(t):
        nb = T.nb[:, t * K:(t + 1) * K]
        hi = T.lm[:, 2 * t * K:(2 * t + 1) * K]
        cp(hi, nb, ["nb%d" % t], ["lh%d" % t])
        tt(T.lm[:, (2 * t + 1) * K:(2 * t + 2) * K], nb, hi, A.subtract, ["nb%d" % t, "lh%d" % t], ["ll%d" % t])
        allsend("l", t, [(T.lm[:, 2 * t * K:(2 * t + 2) * K], T.ld[t * N + q])], ["lh%d" % t, "ll%d" % t])

    def link_table(t):
        it = []
        for p in [q] + peers:
            src = T.lm[:, 2 * t * K:(2 * t + 2) * K] if p == q else T.ld[t * N + p]
            r = ["lh%d" % t, "ll%d" % t] if p == q else ["l%d_%d" % (t, p)]
            for h in range(2):
                o = K - h * K + p * 2 * S
                it.append((T.lt[h::16, o:o + 2 * S], src, r))
        dmas("dl", it, ["lt"])

    def two_send(kind, t, a, b, dram, r):
        allsend(kind, t, [(a, dram[(t * N + q) * 2]), (b, dram[(t * N + q) * 2 + 1])], r)

    def two_table(kind, t, a, b, dram, r0, tab, h0, sem, w):
        it = []
        for p in [q] + peers:
            for h in range(2):
                src = (a, b)[h] if p == q else dram[(t * N + p) * 2 + h]
                it.append((tab[h0 + h::16, p * S:(p + 1) * S], src, r0 if p == q else ["%s%d_%d" % (kind, t, p)]))
        dmas(sem, it, w)

    col = lambda buf, t: buf[:, t * K:(t + 1) * K]
    sm = lambda i: col(T.s, i)
    pd, pe_, kb, kd = [col(T.pg, i) for i in range(4)]
    ke, pgn, pav = T.pa[:, :K], T.pv[:, :K], T.pv[:, K:2 * K]
    one = T.pf[:, 20:21]

    def m_make(t):
        tt(col(T.mf, t), col(T.cf, t), T.vf[:], A.min, ["cf", "vf"], ["mf%d" % t])
        cp(col(T.mh, t), col(T.mf, t), ["mf%d" % t], ["mh%d" % t])
        tt(col(T.ml, t), col(T.mf, t), col(T.mh, t), A.subtract, ["mf%d" % t, "mh%d" % t], ["ml%d" % t])

    def m_send(t):
        two_send("m", t, col(T.mh, t), col(T.ml, t), T.md, ["mh%d" % t, "ml%d" % t])

    def m_table(t):
        two_table("m", t, col(T.mh, t), col(T.ml, t), T.md, ["mh%d" % t, "ml%d" % t], T.kt, 1, "dm", ["ktm"])

    def c_place(t):
        place(col(T.cf, t), K, col(T.cp, t), ["cf"], ["cp%d" % t], 2 * K, K)

    def link_gather(t):
        act(T.lg[:], T.lt[:, :].indirect(col(T.cp, t)), F.Copy, ["lt", "cp%d" % t], ["lg"])

    def d_use(t):
        hi, lo = col(T.dm, 2 * t), col(T.dm, 2 * t + 1)
        fold(pd, T.bl, T.lg, 0, True, True, ["bl", "lg"], ["pd"], "g")
        cp(T.dn[:], pd, ["pd"], ["dn"], ["g"])
        cp(hi, pd, ["pd"], ["dh%d" % t], ["g"])
        cp(T.de[:, :K], pd, ["pd"], ["de0"], ["g"])
        tt(lo, pd, hi, A.subtract, ["pd", "dh%d" % t], ["dlo%d" % t], ["g"])
        r = ["dh%d" % t, "dlo%d" % t]
        two_send("d", t, hi, lo, T.dd, r)
        two_table("d", t, hi, lo, T.dd, r, T.lt, 0, "dd", ["lt"])

    def open_e():
        for z in "ba":
            mm([(PS[z][:, a:b], T.ip[:], T.xv[:, a:b], True, False) for a, b in CH], ["ip", "xv"], ["ps" + z], banks3(z))

    H = S // 2
    dmas("ldl", [(T.li[:], T.link[:], [])], ["li"], "S")
    dmas("ldx0", [(T.xraw[:, :H], T.x[:, :H], [])], ["xr0"])
    dmas("ldx1", [(T.xraw[:, H:], T.x[:, H:], [])], ["xr1"], "S")
    dmas("ldu", [(T.uraw[:], T.u[:], [])], ["ur"])
    dmas("ldc", [(T.ci[:], T.cand[:], [])], ["ci"])
    op("G", lambda: g.iota(T.pi[:, 0:1], [[0, 1]], 0, 1), [], ["pi0"])
    op("G", lambda: g.iota(T.row[:], [[1, 144]], -15, 0, allow_small_or_imprecise_dtypes=True), [], ["row"])
    op("G", lambda: g.iota(T.rowi[:], [[1, 128]], 16, 0), [], ["rowi"])
    op("G", lambda: g.iota(T.vk[:], [[16, K]], q * S, 0, allow_small_or_imprecise_dtypes=True), [], ["vk"])
    gfill = lambda p: op("G", lambda: g.iota(blk(T.kt, 0, p), [[0, S]], 0, 0, allow_small_or_imprecise_dtypes=True), [], ["kf"])
    sfill = lambda p: act(blk(T.kt, 0, p), T.xraw[:], F.Copy, ["xr0", "xr1"], ["ktm"])

    fill(T.lt[:, :4096], 0.0, ["lt_a"])
    cp(T.nb[:, :K], T.li[:], ["li"], ["nb0"])
    link_msg(0)
    for h in range(2):
        own = T.xt[:, q * S + h * H:q * S + (h + 1) * H]
        act(own, T.xraw[:, h * H:(h + 1) * H], F.Copy, ["xr%d" % h], ["xo%d" % h], scale=1.0 / 16)
        send([(cores[sib], se, "xs%d" % h, own, own), (cores[f0], fe, "xf%d" % h, own, own)], ["xo%d" % h])
    wr["xt0_%d" % q] = wr["xo1"]
    wr["xt0_%d" % sib] = [("xs0", len(se)), ("xs1", len(se))]
    wr["xt0_%d" % f0] = [("xf0", len(fe)), ("xf1", len(fe))]
    wr["xt0_%d" % f1] = [("xw0", len(se)), ("xw1", len(se))]
    gfill(0)
    for h in range(2):
        wait("G", [("xf%d" % h, len(fe))])
        a = T.xt[:, f0 * S + h * H:f0 * S + (h + 1) * H]
        send([(cores[sib], se, "xw%d" % h, a, a)], [])
    gfill(1)
    sfill(2)
    cp(T.pf[:, 0:1], T.pi[:, 0:1], ["pi0"], ["p"])
    ts(T.pi[:, 4:5], T.pi[:, 0:1], 15, None, A.bitwise_and, None, ["pi0"], ["pi4"])
    fill(T.pf[:, 28:29], -31.0 / 32, ["pfs"])
    fill(one, 1.0, ["pf1"])
    ts(T.ip[:], T.row[:, 15:143], T.pf[:, 0:1], None, A.is_equal, None, ["row", "p"], ["ip"])
    ts(T.im[:], T.row[:, 15:143], T.pf[:, 0:1], -1.0, A.is_equal, A.mult, ["row", "p"], ["im"])
    fill(T.lt[:, 4096:6144], 0.0, ["lt_b"])
    ts(T.ut[:], T.uraw[:], 1.0 / 16, -1.0, A.mult, A.add, ["ur"], ["ut"])
    fill(T.lt[:, 6144:], 0.0, ["lt"])
    link_table(0)
    wait("S", wr["pfs"] + wr["pf1"])
    tab_sign(1)
    sfill(3)
    tab_end(1)
    tab_send(1)
    wr["ktm"] = wr["ktm"] + wr["kf"]
    wr["ktk"] = wr["ktm"]
    cp(T.cf[:], T.ci[:], ["ci"], ["cf"])
    cp(T.pf[:, 4:5], T.pi[:, 4:5], ["pi4"], ["pm"])
    c_place(0)
    link_gather(0)
    tt(T.pf[:, 8:9], T.pf[:, 0:1], T.pf[:, 4:5], A.subtract, ["p", "pm"], ["g16"])
    ts(T.pf[:, 12:13], T.pf[:, 4:5], 2.0, None, A.is_lt, None, ["pm"], ["wl"])
    ts(T.vf[:], T.vk[:], T.pf[:, 4:5], None, A.add, None, ["vk", "pm"], ["vf"])
    ts(T.bl[:], T.row[:], T.pf[:, 8:9], T.pf[:, 12:13], A.is_equal, A.mult, ["row", "g16", "wl"], ["bl"])
    ts(T.xv[:], T.xraw[:], 1.0 / 16, None, A.mult, None, ["xr0", "xr1"], ["xv"])
    open_e()
    m_make(0)
    m_send(0)
    m_table(0)
    cp(T.bn[:], T.li[:], ["li"], ["bn"])
    cp(T.cn[:], T.ci[:], ["ci"], ["cn"])
    ts(T.bp[:], T.row[:], T.pf[:, 8:9], 16.0, A.is_equal, A.mult, ["row", "g16"], ["bp"])
    ts(T.bm[:], T.row[:], T.pf[:, 8:9], -16.0, A.is_equal, A.mult, ["row", "g16"], ["bm"])
    place(T.nb[:, :K], K, T.ko[:, :K], ["nb0"], ["ko0"], K, 0)
    d_use(0)

    def late_start():
        ts(T.pf[:, 13:14], T.pf[:, 4:5], 0.0, 16385.0, A.is_equal, A.mult, ["pm"], ["wk0"])
        ts(T.pf[:, 14:15], T.pf[:, 4:5], 3.0, None, A.is_lt, None, ["pm"], ["wk1"])
        ts(T.rowj[:], T.rowi[:], 127, None, A.bitwise_and, None, ["rowi"], ["rowj"])
        cp(T.vd[:, :K], T.vf[:], ["vf"], ["vh"])
        tt(T.pf[:, 16:17], T.pf[:, 13:14], T.pf[:, 14:15], A.subtract, ["wk0", "wk1"], ["wk"])
        ts(T.sh[:], T.rowj[:], T.pf[:, 0:1], float(W), A.is_equal, A.mult, ["rowj", "p"], ["sh"])
        tt(T.vd[:, K:], T.vf[:], T.vd[:, :K], A.subtract, ["vf", "vh"], ["vl"])
        ts(T.bk[:], T.row[:], T.pf[:, 8:9], T.pf[:, 16:17], A.is_equal, A.mult, ["row", "g16", "wk"], ["bk"])

    for t in range(RO):
        nb = col(T.nb, t)
        last = t == RO - 1
        u = t + 1
        if t == 0:
            X, xr = T.xt, ["xt0_%d" % p for p in range(N)]
        else:
            X, xr = T.xc, ["xc_own", "xc_V", "xc_S"]
            cols = [c for p in range(N) if p != q for c in range(p * K, (p + 1) * K)]
            tabs = ["xt%d_%d" % (n, p) for n in range(t + 1) for p in range(N)]
            for e, part in (("V", cols[:112]), ("S", cols[112:])):
                runs = []
                for c in part:
                    if runs and runs[-1][1] == c:
                        runs[-1][1] = c + 1
                    else:
                        runs.append([c, c + 1])
                for a, b in runs:
                    src = T.xt[:, :(t + 1) * W].indirect(T.av[:, t * N * K + a:t * N * K + b])
                    r = tabs + ["a%d_%d" % (t, p) for p in range(a // K, (b - 1) // K + 1)]
                    if e == "V":
                        cp(T.xc[:, 16 * a:16 * b], src, r, ["xc_V"])
                    else:
                        act(T.xc[:, 16 * a:16 * b], src, F.Copy, r, ["xc_S"])
            link_gather(t)
        win = X[:, :W]
        term = lambda z, y, yr: mm([(PS[z][:, a:b], T.ip[:], y[:, a:b], False, False) for a, b in CH], ["ip", yr], ["ps" + z], banks3(z))
        xdt = lambda z, i: mm([(PS[z][:, CH[i][0]:CH[i][1]], T.im[:], T.xd[:, CH[i][0]:CH[i][1]], False, True)],
                              ["im", "xd%d" % i], ["e%s%d" % (z, i)], [z + str(i)])
        gf = lambda B, src, r, first=False, end=False: fold(pgn, B, src, 0, first, end, ["bp", "bm"] + r, ["pgn"], "v")
        ck = t * K
        tt(T.yb[:], win.indirect(T.bn[:]), T.xv[:], A.subtract, xr + ["bn", "xv"], ["yb"])
        term("b", T.yb, "yb")
        ts(T.p1[:], T.yb[:], -1.0, None, A.max, None, ["yb"], ["p1"])
        gf(T.bm, T.p1, ["p1"], True)
        ts(T.c1[:], T.yb[:], 0.0, 1.0, A.max, A.min, ["yb"], ["c1"])
        tt(T.yc[:, :H], win.indirect(T.cn[:, ck:ck + K // 2]), T.xv[:, :H], A.subtract, xr + ["cn", "xv"], ["yc"])
        if t > 0:
            d_use(t)
        gf(T.bp, T.c1, ["c1"])
        tt(T.yc[:, H:], win.indirect(T.cn[:, ck + K // 2:ck + K]), T.xv[:, H:], A.subtract, xr + ["cn", "xv"], ["yc"])
        for i, (a, b) in enumerate(CH):
            act(T.xd[:, a:b], win.indirect(T.dn[:, a // 16:b // 16]), F.Copy, xr + ["dn"], ["xd%d" % i])
        ts(T.p3[:], T.yc[:], -1.0, None, A.max, None, ["yc"], ["p3"])
        ts(T.c3[:], T.yc[:], 0.0, 1.0, A.max, A.min, ["yc"], ["c3"])
        xdt("b", 0)
        term("a", T.yc, "yc")
        xdt("b", 1)
        xdt("b", 2)
        gf(T.bp, T.p3, ["p3"])
        for i in range(3):
            xdt("a", i)
        gf(T.bm, T.c3, ["c3"])
        for z, i in (("b", 0), ("b", 1), ("b", 2), ("a", 0), ("a", 1), ("a", 2)):
            a, b = CH[i]
            pz, cz, nm = (T.p4, T.c4, "4_%d" % i) if z == "b" else (T.p2, T.c2, "2_%d" % i)
            act(pz[:, a:b], PS[z][:, a:b], F.Relu, ["e%s%d" % (z, i)], ["p" + nm], [z + str(i)], bias=one)
            if i == 1:
                ts(cz[:, :b], pz[:, :b], 1.0, 2.0, A.max, A.min, ["p" + nm], ["c" + nm])
            if i == 2:
                ts(cz[:, a:b], pz[:, a:b], 1.0, 2.0, A.max, A.min, ["p" + nm], ["c" + nm])
                w_ = (T.bp, T.bm) if z == "b" else (T.bm, T.bp)
                gf(w_[0], pz, ["p" + nm])
                gf(w_[1], cz, ["c" + nm], False, z == "a")
        km = col(T.km, t)
        if not last:
            m_make(u)
        ts(km, pgn, 0.0, None, A.max, None, ["pgn"], ["km%d" % t], ["v"])
        allsend("k", t, [(km, T.kd[t * N + q])], ["km%d" % t])
        dmas("dk", [(T.kt[0::16, p * S:(p + 1) * S], km if p == q else T.kd[t * N + p],
                     ["km%d" % t] if p == q else ["k%d_%d" % (t, p)]) for p in [q] + peers], ["ktk"])
        if not last:
            wait("G", wr["ktk"])
            m_send(u)
        act(T.lg[:], T.lt[:, :W].indirect(T.ko[:, :K]), F.Copy, ["lt", "ko0"], ["lg"])
        fold(pe_, T.bl, T.lg, 0, True, True, ["bl", "lg"], ["pe"], "g")
        if t + 2 < RO:
            tab_sign(t + 2)
        ts(sm(11), km, 16384.0, None, A.mult, None, ["km%d" % t], ["s11"])
        ts(sm(1), km, 32768.0, -6000.0, A.mult, A.add, ["km%d" % t], ["s1"])
        tt(sm(4), col(T.cf, t), nb, A.subtract, ["cf", "nb%d" % t], ["s4"])
        tt(sm(0), sm(11), col(T.mf, t), A.subtract, ["s11", "mf%d" % t], ["s0"])
        cp(T.de[:, K:], pe_, ["pe"], ["de1"], ["g"])
        ts(sm(2), sm(0), 0.0, None, A.max, None, ["s0"], ["s2"])
        place(T.de[:], 2 * K, T.ko[:, K:], ["de0", "de1"], ["ko1"], K, 0)
        tt(sm(3), sm(0), sm(1), A.min, ["s0", "s1"], ["s3"])
        tt(sm(5), T.de[:, K:], nb, A.subtract, ["de1", "nb%d" % t], ["s5"])
        if t == 0:
            late_start()
        if not last:
            c_place(u)
        kr = ["ktm", "ktk", "ko0", "ko1"]
        kw = T.kt[:, :]
        cp(T.kg[:, :S], kw.indirect(T.ko[:, :K]), kr, ["kg0"])
        act(T.kg[:, S:2 * S], kw.indirect(T.ko[:, K:2 * K]), F.Copy, kr, ["kg1"])
        cp(T.kg[:, 2 * S:2 * S + H], kw.indirect(T.ko[:, 2 * K:2 * K + K // 2]), kr, ["kg2"])
        act(T.kg[:, 2 * S + H:], kw.indirect(T.ko[:, 2 * K + K // 2:]), F.Copy, kr, ["kg3"])
        if t + 2 < RO:
            tab_end(t + 2)
        if not last:
            hist = [(T.ip, T.vd[:, :K]), (T.ip, T.vd[:, K:])] + [(T.sh, col(T.go, i)) for i in range(2 * t)]
            mm([(pav, B[:], x_, i == 0, False) for i, (B, x_) in enumerate(hist)], ["ip", "sh", "vh", "vl"], ["pav"], ["v"])
        fold(kb, T.bk, T.kg, 0, True, True, ["bk", "kg0"], ["kb"], "g")
        fold(kd, T.bk, T.kg, S, True, True, ["bk", "kg1"], ["kd"], "g")
        fold(ke, T.bk, T.kg, 2 * S, True, True, ["bk", "kg2", "kg3"], ["ke"], "a0")
        gv, gb = col(T.go, 2 * t), col(T.go, 2 * t + 1)
        gn, hn = "gv%d" % t, "gb%d" % t
        tt(sm(6), kb, sm(3), A.is_lt, ["kb", "s3"], ["s6"], ["g"])
        tt(sm(7), kd, sm(3), A.is_lt, ["kd", "s3"], ["s7"], ["g"])
        tt(gv, sm(6), sm(7), A.mult, ["s6", "s7"], [gn])
        tt(sm(9), gv, sm(4), A.mult, [gn, "s4"], ["s9"])
        tt(sm(8), ke, sm(2), A.max, ["ke", "s2"], ["s8"], ["a0"])
        tt(sm(11), sm(9), nb, A.add, ["s9", "nb%d" % t], ["s11"])
        tt(gb, kb, sm(8), A.is_gt, ["kb", "s8"], [hn], ["g"])
        if not last:
            mm([(pav, T.sh[:], gv, False, False), (pav, T.sh[:], gb, False, True)], [gn, hn], ["pav"], ["v"])
        tt(sm(10), gb, sm(5), A.mult, [hn, "s5"], ["s10"])
        if not last:
            avo = T.av[:, u * N * K + q * K:u * N * K + (q + 1) * K]
            cp(avo, pav, ["pav"], ["avo%d" % u], ["v"])
            allsend("a", u, [(avo, avo)], ["avo%d" % u])
        new = col(T.nb, u)
        tt(new, sm(11), sm(10), A.add, ["s11", "s10"], ["nb%d" % u])
        if last:
            break
        link_msg(u)
        link_table(u)
        if u + 1 < RO:
            wait("G", wr["lt"])
            tab_send(u + 1)
        m_table(u)
        tabs = ["xt%d_%d" % (n, p) for n in range(u + 1) for p in range(N)]
        act(T.xc[:, q * S:(q + 1) * S], T.xt[:, :(u + 1) * W].indirect(avo), F.Copy, tabs + ["avo%d" % u], ["xc_own"])
        cp(T.bn[:], new, ["nb%d" % u], ["bn"])
        place(new, K, T.ko[:, :K], ["nb%d" % u], ["ko0"], K, 0)
        cp(T.xv[:], T.xc[:, q * S:(q + 1) * S], ["xc_own"], ["xv"])
        open_e()

    dmas("out", [(T.ylink[:], T.nb[:, RO * K:], ["nb%d" % RO])], ["y"])
    wait("G", [(k, cnt[k]) for k in ("ls", "V", "S", "P", "G", "out")])
